import numpy as np
import ml_dtypes


def mxq(x, axis, fmt="e4m3"):
    dtype, down = {"e4m3": (ml_dtypes.float8_e4m3fn, 7), "e5m2": (ml_dtypes.float8_e5m2, 14)}[fmt]
    v = np.moveaxis(np.asarray(x, np.float32).astype(ml_dtypes.bfloat16).astype(np.float64), axis, -1)
    blocks = v.reshape(v.shape[:-1] + (-1, 32))
    amax = np.abs(blocks).max(-1, keepdims=True)
    byte = np.maximum(np.where(amax > 0, np.frexp(amax)[1] - 1 + 127, 0) - down, 1)
    scale = np.exp2(byte - 127.0)
    codes = (blocks / scale).astype(np.float32).astype(dtype).astype(np.float64)
    return np.moveaxis((codes * scale).reshape(v.shape), -1, axis)


WIDE = False


def mx_kscale(k):
    if not WIDE:
        return np.ones(k)
    levels = np.array([10, -10, 5, -5, 0])
    if k % 512:
        return np.exp2(np.random.permutation(np.resize(levels, k // 32))).repeat(32)
    a = np.empty((k // 512, 16))
    for p in range(k // 512):
        a[p, :8] = np.random.permutation(np.resize(levels, 8))
        for g in range(8):
            far = levels[np.abs(levels - a[p, g]) >= 10]
            a[p, g + 8] = far[np.random.randint(len(far))]
    return np.exp2(a.ravel()).repeat(32)


def f64(x):
    return np.asarray(x).astype(np.float64)


def striped(idx):
    return np.tile(idx.reshape(-1, 16).T, (8, 1)).astype(np.uint16)


def unstriped(offs):
    return offs[:16].T.reshape(-1).astype(np.int64)


E2M1 = np.array([0.0, 0.5, 1.0, 1.5, 2.0, 3.0, 4.0, 6.0, -0.0, -0.5, -1.0, -1.5, -2.0, -3.0, -4.0, -6.0])


def pack_weight(w, fmt):
    k, n = w.shape
    w = f64(np.asarray(w, np.float32).astype(ml_dtypes.bfloat16)).reshape(k // 32, 32, n)
    amax = np.abs(w).max(1)
    if fmt == "e4m3":
        byte = np.frexp(amax)[1] - 1 + 127 - 7
    else:
        mant, ex = np.frexp(amax / 6.0)
        byte = np.where(mant > 0.5, ex, ex - 1) + 127
    byte = np.clip(np.where(amax > 0, byte, 1), 1, 254)
    scaled = (w * np.exp2(127.0 - byte)[:, None, :]).reshape(k, n).astype(np.float32)
    by_word = np.ascontiguousarray(scaled.reshape(k // 512, 128, 4, n).transpose(0, 1, 3, 2))
    if fmt == "e4m3":
        words = by_word.astype(ml_dtypes.float8_e4m3fn).view(np.uint8)
    else:
        c = by_word.astype(ml_dtypes.float4_e2m1fn).view(np.uint8) & 0xF
        words = (c[..., 0::2] | (c[..., 1::2] << 4)).reshape(k // 512, 128, 2 * n)
    return np.ascontiguousarray(words), np.ascontiguousarray(byte.astype(np.uint8).reshape(k // 512, 16, n))


def unpack_weight(words, scales, fmt):
    g, _, n = scales.shape
    words = np.ascontiguousarray(words).reshape(g, 128, n, -1)
    if fmt == "e4m3":
        vals = words.view(ml_dtypes.float8_e4m3fn).astype(np.float64)
    else:
        nib = np.empty((g, 128, n, 4), np.uint8)
        nib[..., 0::2] = words & 0xF
        nib[..., 1::2] = words >> 4
        vals = E2M1[nib]
    vals = vals * np.repeat(np.exp2(scales.astype(np.float64) - 127.0), 8, axis=1)[..., None]
    return vals.transpose(0, 1, 3, 2).reshape(g * 512, n)


def gelu(v):
    return 0.5 * v * (1.0 + np.tanh(np.sqrt(2.0 / np.pi) * (v + 0.044715 * v**3)))


K, T, E, C, H, N = 1536, 1024, 4, 256, 512, 128
R = 2


def by_expert(wq, xq):
    return np.concatenate([wq[e].T @ xq[:, e * C:(e + 1) * C] for e in range(E)], axis=1)


def setup_inputs():
    n = np.random.standard_normal
    s = mx_kscale(K)[:, None]
    u = mx_kscale(H)
    slot_token = np.concatenate([r * (T // R) + np.random.permutation(T // R)[:C // R] for e in range(E) for r in range(R)])
    x = pack_weight(n((K, T)) * s, "e4m3")
    return {
        "x_words": x[0],
        "x_scales": x[1],
        "w1": (n((E, K, H)) / np.sqrt(K) / s[None]).astype(np.float32),
        "w3": (n((E, K, H)) / np.sqrt(K) / s[None] * u[None, None, :]).astype(np.float32),
        "w2": (n((E, H, N)) / np.sqrt(H) / u[None, :, None]).astype(np.float32),
        "offs": striped(slot_token),
    }


def reference(x_words, x_scales, w1, w3, w2, offs):
    idx = unstriped(offs)
    xq = unpack_weight(x_words, x_scales, "e4m3")[:, idx]
    h = gelu(by_expert(mxq(f64(w1), 1, "e4m3"), xq))
    h = h * by_expert(mxq(f64(w3), 1, "e4m3"), xq)
    y = by_expert(mxq(f64(w2), 1, "e4m3"), mxq(h, 0, "e4m3"))
    return y.reshape(N, E, R, C // R).transpose(0, 2, 1, 3).reshape(N, E * C)

@@ -1,0 +1,176 @@
+from contextlib import ExitStack
+
+import concourse.mybir as mybir
+
+K, T, E, C, H, N = 1536, 1024, 4, 256, 512, 128
+RANKS = 2
+FLOPS = 2 * E * C * (2 * K * H + H * N)
+
+F32 = mybir.dt.float32
+BF16 = mybir.dt.bfloat16
+I32 = mybir.dt.int32
+U32 = mybir.dt.uint32
+U16 = mybir.dt.uint16
+U8 = mybir.dt.uint8
+FP8X4 = mybir.dt.float8_e4m3fn_x4
+GELU = mybir.ActivationFunctionType.Gelu_apprx_tanh
+MULT = mybir.AluOpType.mult
+
+P = 128
+PACK = 4
+K_PASS = P * PACK
+PASSES = K // K_PASS
+HALF = C // RANKS
+VECTOR_SHARE = 48
+VECTOR_SHARE_LAST = 84
+
+
+def tile_moe_pke_glu_gelu_kernel(tc, x_words, x_scales, w1, w3, w2, offs, out):
+    nc = tc.nc
+    with ExitStack() as ctx:
+        keep = ctx.enter_context(tc.tile_pool(name="keep", bufs=1))
+        raws = ctx.enter_context(tc.tile_pool(name="raws", bufs=12))
+        ring = ctx.enter_context(tc.tile_pool(name="ring", bufs=4))
+        psum = ctx.enter_context(tc.psum_pool(name="psum", bufs=1))
+        psum_y = ctx.enter_context(tc.psum_pool(name="psum_y", bufs=4))
+
+        offsets = keep.tile([P, E * C // 16], U16, name="offsets")
+        nc.sync.dma_start(offsets[:], offs)
+
+        token_scales = keep.tile([P, T], U8, name="token_scales", align_bytes=64)
+        nc.vector.memset(token_scales[:].bitcast(I32), 0)
+        for q in range(4):
+            nc.scalar.dma_start(
+                out=token_scales[32 * q : 32 * q + 4 * PASSES, :].bitcast(I32),
+                in_=x_scales[:, 4 * q : 4 * q + 4, :].bitcast(I32),
+            )
+        token_words = []
+        for o in range(PASSES):
+            words = keep.tile([P, T], I32, name="token_words%d" % o, align_bytes=64)
+            nc.sync.dma_start(out=words[:], in_=x_words[o].rearrange("p t r -> p (t r)").bitcast(I32))
+            token_words.append(words)
+
+        def gather(e):
+            picks = offsets[:, e * C // 16 : (e + 1) * C // 16]
+            slot_words = []
+            for o in range(PASSES):
+                gathered = keep.tile([P, C], U32, name="slot_words%d_%d" % (e, o), align_bytes=64)
+                nc.vector.tensor_copy(gathered[:], token_words[o][:].bitcast(U32).indirect(picks))
+                slot_words.append(gathered)
+            slot_scales = keep.tile([P, C], U8, name="slot_scales%d" % e, align_bytes=64)
+            nc.vector.tensor_copy(slot_scales[:], token_scales[:].indirect(picks))
+            return slot_words, slot_scales
+
+        def first_layer(w, e, slots, tag, last):
+            slot_words, slot_scales = slots
+            banks = [psum.tile([P, PACK, HALF], F32, name="%s%d" % (tag, m)) for m in range(RANKS)]
+            for o in range(PASSES):
+                final = last and o == PASSES - 1
+                raw = raws.tile([P, PACK, H], F32, name="raw")
+                nc.sync.dma_start(
+                    out=raw[:], in_=w[e, o * K_PASS : (o + 1) * K_PASS, :].rearrange("(p j) c -> p j c", j=PACK)
+                )
+                grouped = ring.tile([P, PACK * H], BF16, name="grouped", align_bytes=64)
+                src = raw[:].rearrange("p j (m t) -> p m j t", t=PACK)
+                dst = grouped[:].rearrange("p (t m j) -> p m j t", t=PACK, j=PACK)
+                cut = VECTOR_SHARE_LAST if final else VECTOR_SHARE
+                nc.scalar.copy(out=dst[:, cut:, :, :], in_=src[:, cut:, :, :])
+                nc.vector.tensor_copy(out=dst[:, :cut, :, :], in_=src[:, :cut, :, :])
+                codes = ring.tile([P, H], U32, name="codes", align_bytes=64)
+                scales = ring.tile([P, H], U8, name="scales", align_bytes=64)
+                width = P if final else H
+                for c0 in range(0, H, width):
+                    nc.vector.quantize_mx(
+                        out=codes[:, c0 : c0 + width].bitcast(FP8X4),
+                        scales=scales[:, c0 : c0 + width],
+                        in_=grouped[:, PACK * c0 : PACK * (c0 + width)],
+                    )
+                for m in range(RANKS):
+                    cols = slice(m * HALF, (m + 1) * HALF)
+                    for t in range(PACK):
+                        nc.tensor.matmul_mx(
+                            out=banks[m][:, t, :],
+                            lhsT=codes[:, t * P : (t + 1) * P].bitcast(FP8X4),
+                            lhsT_scale=scales[:, t * P : (t + 1) * P],
+                            rhs=slot_words[o][:, cols].bitcast(FP8X4),
+                            rhs_scale=slot_scales[4 * o : P, cols],
+                            start=(o == 0 and t == 0),
+                            stop=(o == PASSES - 1 and t == PACK - 1),
+                        )
+            return banks
+
+        hidden = []
+        slots = gather(0)
+        for e in range(E):
+            gate_banks = first_layer(w1, e, slots, "gate", False)
+            acts = []
+            for m in range(RANKS):
+                act = ring.tile([P, HALF, PACK], F32, name="act")
+                nc.scalar.activation(out=act[:], in_=gate_banks[m][:].rearrange("p t u -> p u t"), func=GELU)
+                acts.append(act)
+            next_slots = gather(e + 1) if e + 1 < E else None
+            up_banks = first_layer(w3, e, slots, "up", e == E - 1)
+            slots = next_slots
+            h = ring.tile([P, C, PACK], BF16, name="h", align_bytes=64)
+            for m in range(RANKS):
+                nc.vector.tensor_tensor(
+                    out=h[:, m * HALF : (m + 1) * HALF, :],
+                    in0=up_banks[m][:].rearrange("p t u -> p u t"),
+                    in1=acts[m][:],
+                    op=MULT,
+                )
+            h_codes = keep.tile([P, C], U32, name="h_codes%d" % e, align_bytes=64)
+            h_scales = keep.tile([P, C], U8, name="h_scales%d" % e, align_bytes=64)
+            for m in range(RANKS):
+                cols = slice(m * HALF, (m + 1) * HALF)
+                nc.vector.quantize_mx(
+                    out=h_codes[:, cols].bitcast(FP8X4),
+                    scales=h_scales[:, cols],
+                    in_=h[:, cols, :].rearrange("p u t -> p (u t)"),
+                )
+            hidden.append((h_codes, h_scales))
+
+        by_rank = out.rearrange("n (m e u) -> n m e u", m=RANKS, e=E)
+        early = keep.tile([P, RANKS, E - 1, HALF], F32, name="early")
+        down = {}
+        for e in [E - 1] + list(range(E - 1)):
+            raw2 = keep.tile([P, PACK, N], F32, name="raw2_%d" % e)
+            nc.sync.dma_start(out=raw2[:], in_=w2[e].rearrange("(p j) n -> p j n", j=PACK))
+            grouped2 = keep.tile([P, N * PACK], BF16, name="grouped2_%d" % e, align_bytes=64)
+            nc.scalar.copy(
+                out=grouped2[:].rearrange("p (c i j) -> p c j i", i=4, j=PACK),
+                in_=raw2[:].rearrange("p j (c i) -> p c j i", i=4),
+            )
+            codes2 = keep.tile([P, N], U32, name="codes2_%d" % e, align_bytes=64)
+            scales2 = keep.tile([P, N], U8, name="scales2_%d" % e, align_bytes=64)
+            nc.vector.quantize_mx(out=codes2[:].bitcast(FP8X4), scales=scales2[:], in_=grouped2[:])
+            down[e] = (codes2, scales2)
+
+        def second_layer(e, cols):
+            codes2, scales2 = down[e]
+            h_codes, h_scales = hidden[e]
+            y = psum_y.tile([P, C], F32, name="y")
+            width = cols.stop - cols.start
+            nc.tensor.matmul_mx(
+                out=y[:, :width],
+                lhsT=codes2[:].bitcast(FP8X4),
+                lhsT_scale=scales2[:],
+                rhs=h_codes[:, cols].bitcast(FP8X4),
+                rhs_scale=h_scales[:, cols],
+                start=True,
+                stop=True,
+            )
+            return y
+
+        for m in range(RANKS):
+            y = second_layer(E - 1, slice(m * HALF, (m + 1) * HALF))
+            late = keep.tile([P, HALF], F32, name="late%d" % m)
+            if m == 0:
+                nc.scalar.copy(out=late[:], in_=y[:, :HALF])
+            else:
+                nc.vector.tensor_copy(out=late[:], in_=y[:, :HALF])
+            nc.sync.dma_start(out=by_rank[:, m, E - 1, :], in_=late[:])
+        for e in range(E - 1):
+            y = second_layer(e, slice(0, C))
+            nc.scalar.copy(out=early[:, :, e, :], in_=y[:].rearrange("p (m u) -> p m u", m=RANKS))
+        nc.sync.dma_start(out=by_rank[:, :, : E - 1, :], in_=early[:])

@@ -21,130 +21,131 @@ PACK = 4
 K_PASS = P * PACK
 PASSES = K // K_PASS
 HALF = C // RANKS
-VECTOR_SHARE = 48
-VECTOR_SHARE_LAST = 84
+GATHER = C
+GATHERS = {0: [(0, 0), (3, 0)], 1: [(1, 0)], 2: [(2, 0)], 3: [(0, 1), (3, 1)], 4: [(1, 1)], 5: [(2, 1)],
+           7: [(0, 2), (3, 2)], 8: [(1, 2)], 9: [(2, 2)], 13: [(0, 3), (3, 3)], 14: [(1, 3)], 15: [(2, 3)]}
+GELU_AFTER = (1, 0, 0, 1)
+SPLIT_SHARE = (48, 44)
+CHUNKS = 2 * E * PASSES
+GROUPS = [(c,) for c in range(CHUNKS)]
+VECTOR_SHARE = [48] * 6 + [72] * 12 + [56, 56, 16, 56, 72]
+LOAD_CUTS = [(), (3,), (3,), (3,), (2, 1), (2, 1), (1, 1, 1), (1, 1)]
 
 
 def tile_moe_pke_glu_gelu_kernel(tc, x_words, x_scales, w1, w3, w2, offs, out):
     nc = tc.nc
     with ExitStack() as ctx:
         keep = ctx.enter_context(tc.tile_pool(name="keep", bufs=1))
-        raws = ctx.enter_context(tc.tile_pool(name="raws", bufs=12))
+        raws = ctx.enter_context(tc.tile_pool(name="raws", bufs=4))
         ring = ctx.enter_context(tc.tile_pool(name="ring", bufs=4))
         psum = ctx.enter_context(tc.psum_pool(name="psum", bufs=1))
         psum_y = ctx.enter_context(tc.psum_pool(name="psum_y", bufs=4))
 
+        def load_passes(raw, w, e, o0, count):
+            rows = w[e].rearrange("(o p j) c -> p o (j c)", o=PASSES, j=PACK)
+            nc.sync.dma_start(out=raw[:, o0 : o0 + count, :], in_=rows[:, o0 : o0 + count, :])
+
+        def load_words(o):
+            words = keep.tile([P, T], I32, name="token_words%d" % o, align_bytes=64)
+            nc.sync.dma_start(out=words[:], in_=x_words[o].rearrange("p t r -> p (t r)").bitcast(I32))
+            return words
+
         offsets = keep.tile([P, E * C // 16], U16, name="offsets")
         nc.sync.dma_start(offsets[:], offs)
+        first_raw = raws.tile([P, PASSES, PACK * H], F32, name="raw")
+        load_passes(first_raw, w1, 0, 0, 1)
+        token_words = [load_words(0)]
+        load_passes(first_raw, w1, 0, 1, 1)
 
         token_scales = keep.tile([P, T], U8, name="token_scales", align_bytes=64)
         nc.vector.memset(token_scales[:].bitcast(I32), 0)
+        landed_scales = keep.tile([P, T // 4], I32, name="landed_scales")
         for q in range(4):
-            nc.scalar.dma_start(
-                out=token_scales[32 * q : 32 * q + 4 * PASSES, :].bitcast(I32),
-                in_=x_scales[:, 4 * q : 4 * q + 4, :].bitcast(I32),
-            )
-        token_words = []
-        for o in range(PASSES):
-            words = keep.tile([P, T], I32, name="token_words%d" % o, align_bytes=64)
-            nc.sync.dma_start(out=words[:], in_=x_words[o].rearrange("p t r -> p (t r)").bitcast(I32))
-            token_words.append(words)
+            live = slice(32 * q, 32 * q + 4 * PASSES)
+            nc.sync.dma_start(out=landed_scales[live, :], in_=x_scales[:, 4 * q : 4 * q + 4, :].bitcast(I32))
+            nc.vector.tensor_copy(out=token_scales[live, :].bitcast(I32), in_=landed_scales[live, :])
+        token_words.append(load_words(1))
+        load_passes(first_raw, w1, 0, 2, 1)
+        token_words.append(load_words(2))
 
-        def gather(e):
-            picks = offsets[:, e * C // 16 : (e + 1) * C // 16]
-            slot_words = []
-            for o in range(PASSES):
-                gathered = keep.tile([P, C], U32, name="slot_words%d_%d" % (e, o), align_bytes=64)
-                nc.vector.tensor_copy(gathered[:], token_words[o][:].bitcast(U32).indirect(picks))
-                slot_words.append(gathered)
-            slot_scales = keep.tile([P, C], U8, name="slot_scales%d" % e, align_bytes=64)
-            nc.vector.tensor_copy(slot_scales[:], token_scales[:].indirect(picks))
-            return slot_words, slot_scales
+        slot_words = [keep.tile([P, E * C], U32, name="slot_words%d" % o, align_bytes=64) for o in range(PASSES)]
+        slot_scales = keep.tile([P, E * C], U8, name="slot_scales", align_bytes=64)
 
-        def first_layer(w, e, slots, tag, last):
-            slot_words, slot_scales = slots
-            banks = [psum.tile([P, PACK, HALF], F32, name="%s%d" % (tag, m)) for m in range(RANKS)]
-            for o in range(PASSES):
-                final = last and o == PASSES - 1
-                raw = raws.tile([P, PACK, H], F32, name="raw")
-                nc.sync.dma_start(
-                    out=raw[:], in_=w[e, o * K_PASS : (o + 1) * K_PASS, :].rearrange("(p j) c -> p j c", j=PACK)
-                )
-                grouped = ring.tile([P, PACK * H], BF16, name="grouped", align_bytes=64)
-                src = raw[:].rearrange("p j (m t) -> p m j t", t=PACK)
-                dst = grouped[:].rearrange("p (t m j) -> p m j t", t=PACK, j=PACK)
-                cut = VECTOR_SHARE_LAST if final else VECTOR_SHARE
+        def gather(gathered, window, piece):
+            picks = offsets[:, piece * GATHER // 16 : (piece + 1) * GATHER // 16]
+            nc.vector.tensor_copy(gathered[:, piece * GATHER : (piece + 1) * GATHER], window.indirect(picks))
+
+        raw_tiles = {0: first_raw}
+        banks = {}
+
+        def cast(chunk, grouped, codes, scales):
+            index, o = divmod(chunk, PASSES)
+            if index not in raw_tiles:
+                raw_tiles[index] = raws.tile([P, PASSES, PACK * H], F32, name="raw")
+                o0 = 0
+                for count in LOAD_CUTS[index]:
+                    load_passes(raw_tiles[index], (w1, w3)[index % 2], index // 2, o0, count)
+                    o0 += count
+            src = raw_tiles[index][:, o, :].rearrange("p (j m t) -> p m j t", j=PACK, t=PACK)
+            dst = grouped.rearrange("p (t m j) -> p m j t", t=PACK, j=PACK)
+            if chunk < CHUNKS - 1:
+                cut = VECTOR_SHARE[chunk]
                 nc.scalar.copy(out=dst[:, cut:, :, :], in_=src[:, cut:, :, :])
                 nc.vector.tensor_copy(out=dst[:, :cut, :, :], in_=src[:, :cut, :, :])
-                codes = ring.tile([P, H], U32, name="codes", align_bytes=64)
-                scales = ring.tile([P, H], U8, name="scales", align_bytes=64)
-                width = P if final else H
-                for c0 in range(0, H, width):
+                nc.vector.quantize_mx(out=codes.bitcast(FP8X4), scales=scales, in_=grouped)
+                return
+            landing = raw_tiles[index][:, o, :].rearrange("p (j c) -> p j c", j=PACK)
+            rows = w3[E - 1, K - K_PASS :, :].rearrange("(p j) c -> p j c", j=PACK)
+            for half in range(2):
+                c0, c1 = half * H // 2, (half + 1) * H // 2
+                nc.sync.dma_start(out=landing[:, :, c0:c1], in_=rows[:, :, c0:c1])
+            for half in range(2):
+                m0, m1 = half * P // 2, (half + 1) * P // 2
+                cut = m0 + SPLIT_SHARE[half]
+                nc.scalar.copy(out=dst[:, cut:m1, :, :], in_=src[:, cut:m1, :, :])
+                nc.vector.tensor_copy(out=dst[:, m0:cut, :, :], in_=src[:, m0:cut, :, :])
+                for t in range(PACK):
+                    w0, w1_ = t * P + m0, t * P + m1
                     nc.vector.quantize_mx(
-                        out=codes[:, c0 : c0 + width].bitcast(FP8X4),
-                        scales=scales[:, c0 : c0 + width],
-                        in_=grouped[:, PACK * c0 : PACK * (c0 + width)],
+                        out=codes[:, w0:w1_].bitcast(FP8X4),
+                        scales=scales[:, w0:w1_],
+                        in_=grouped[:, PACK * w0 : PACK * w1_],
                     )
-                for m in range(RANKS):
-                    cols = slice(m * HALF, (m + 1) * HALF)
-                    for t in range(PACK):
-                        nc.tensor.matmul_mx(
-                            out=banks[m][:, t, :],
-                            lhsT=codes[:, t * P : (t + 1) * P].bitcast(FP8X4),
-                            lhsT_scale=scales[:, t * P : (t + 1) * P],
-                            rhs=slot_words[o][:, cols].bitcast(FP8X4),
-                            rhs_scale=slot_scales[4 * o : P, cols],
-                            start=(o == 0 and t == 0),
-                            stop=(o == PASSES - 1 and t == PACK - 1),
-                        )
-            return banks
 
-        hidden = []
-        slots = gather(0)
-        for e in range(E):
-            gate_banks = first_layer(w1, e, slots, "gate", False)
-            acts = []
-            for m in range(RANKS):
-                act = ring.tile([P, HALF, PACK], F32, name="act")
-                nc.scalar.activation(out=act[:], in_=gate_banks[m][:].rearrange("p t u -> p u t"), func=GELU)
-                acts.append(act)
-            next_slots = gather(e + 1) if e + 1 < E else None
-            up_banks = first_layer(w3, e, slots, "up", e == E - 1)
-            slots = next_slots
-            h = ring.tile([P, C, PACK], BF16, name="h", align_bytes=64)
-            for m in range(RANKS):
-                nc.vector.tensor_tensor(
-                    out=h[:, m * HALF : (m + 1) * HALF, :],
-                    in0=up_banks[m][:].rearrange("p t u -> p u t"),
-                    in1=acts[m][:],
-                    op=MULT,
-                )
-            h_codes = keep.tile([P, C], U32, name="h_codes%d" % e, align_bytes=64)
-            h_scales = keep.tile([P, C], U8, name="h_scales%d" % e, align_bytes=64)
-            for m in range(RANKS):
-                cols = slice(m * HALF, (m + 1) * HALF)
-                nc.vector.quantize_mx(
-                    out=h_codes[:, cols].bitcast(FP8X4),
-                    scales=h_scales[:, cols],
-                    in_=h[:, cols, :].rearrange("p u t -> p (u t)"),
-                )
-            hidden.append((h_codes, h_scales))
+        def multiply(chunk, codes, scales):
+            index, o = divmod(chunk, PASSES)
+            e = index // 2
+            if o == 0:
+                tag = ("gate", "up")[index % 2]
+                banks[index] = [psum.tile([P, PACK, HALF], F32, name="%s%d" % (tag, m)) for m in range(RANKS)]
+            order = [(m, t) for m in range(RANKS) for t in range(PACK)]
+            for m, t in order:
+                cols = slice(e * C + m * HALF, e * C + (m + 1) * HALF)
+                if True:
+                    nc.tensor.matmul_mx(
+                        out=banks[index][m][:, t, :],
+                        lhsT=codes[:, t * P : (t + 1) * P].bitcast(FP8X4),
+                        lhsT_scale=scales[:, t * P : (t + 1) * P],
+                        rhs=slot_words[o][:, cols].bitcast(FP8X4),
+                        rhs_scale=slot_scales[4 * o : P, cols],
+                        start=(o == 0 and t == 0),
+                        stop=(o == PASSES - 1 and t == PACK - 1),
+                    )
 
         by_rank = out.rearrange("n (m e u) -> n m e u", m=RANKS, e=E)
-        early = keep.tile([P, RANKS, E - 1, HALF], F32, name="early")
-        down = {}
-        for e in [E - 1] + list(range(E - 1)):
-            raw2 = keep.tile([P, PACK, N], F32, name="raw2_%d" % e)
-            nc.sync.dma_start(out=raw2[:], in_=w2[e].rearrange("(p j) n -> p j n", j=PACK))
+
+        def down_weights(e, raw2):
+            nc.sync.dma_start(out=raw2, in_=w2[e].rearrange("(p j) n -> p j n", j=PACK))
             grouped2 = keep.tile([P, N * PACK], BF16, name="grouped2_%d" % e, align_bytes=64)
-            nc.scalar.copy(
+            copy = nc.vector.tensor_copy if e == 1 else nc.scalar.copy
+            copy(
                 out=grouped2[:].rearrange("p (c i j) -> p c j i", i=4, j=PACK),
-                in_=raw2[:].rearrange("p j (c i) -> p c j i", i=4),
+                in_=raw2.rearrange("p j (c i) -> p c j i", i=4),
             )
             codes2 = keep.tile([P, N], U32, name="codes2_%d" % e, align_bytes=64)
             scales2 = keep.tile([P, N], U8, name="scales2_%d" % e, align_bytes=64)
             nc.vector.quantize_mx(out=codes2[:].bitcast(FP8X4), scales=scales2[:], in_=grouped2[:])
-            down[e] = (codes2, scales2)
+            return codes2, scales2
 
         def second_layer(e, cols):
             codes2, scales2 = down[e]
@@ -162,15 +163,68 @@ def tile_moe_pke_glu_gelu_kernel(tc, x_words, x_scales, w1, w3, w2, offs, out):
             )
             return y
 
+        down = {}
+        hidden = []
+        acts = {}
+
+        def activate(e):
+            acts[e] = []
+            for m in range(RANKS):
+                act = raw_tiles[2 * e + 1][:, GELU_AFTER[e], m * H : (m + 1) * H].rearrange("p (u t) -> p u t", t=PACK)
+                nc.scalar.activation(out=act, in_=banks[2 * e][m][:].rearrange("p t u -> p u t"), func=GELU)
+                acts[e].append(act)
+
+        def gate(e):
+            h = ring.tile([P, C, PACK], BF16, name="h", align_bytes=64)
+            for m in range(RANKS):
+                nc.vector.tensor_tensor(
+                    out=h[:, m * HALF : (m + 1) * HALF, :],
+                    in0=banks[2 * e + 1][m][:].rearrange("p t u -> p u t"),
+                    in1=acts[e][m],
+                    op=MULT,
+                )
+            h_codes = keep.tile([P, C], U32, name="h_codes%d" % e, align_bytes=64)
+            h_scales = keep.tile([P, C], U8, name="h_scales%d" % e, align_bytes=64)
+            for m in range(RANKS):
+                cols = slice(m * HALF, (m + 1) * HALF)
+                nc.vector.quantize_mx(
+                    out=h_codes[:, cols].bitcast(FP8X4),
+                    scales=h_scales[:, cols],
+                    in_=h[:, cols, :].rearrange("p u t -> p (u t)"),
+                )
+            hidden.append((h_codes, h_scales))
+
+        for chunk in range(CHUNKS):
+            grouped = ring.tile([P, PACK * H], BF16, name="grouped", align_bytes=64)
+            codes = ring.tile([P, H], U32, name="codes", align_bytes=64)
+            scales = ring.tile([P, H], U8, name="scales", align_bytes=64)
+            cast(chunk, grouped[:], codes[:], scales[:])
+            for kind, e in GATHERS.get(chunk, []):
+                if kind < PASSES:
+                    gather(slot_words[kind], token_words[kind][:].bitcast(U32), e)
+                else:
+                    gather(slot_scales, token_scales[:], e)
+            multiply(chunk, codes[:], scales[:])
+            e, place = divmod(chunk, 2 * PASSES)
+            if place == PASSES + GELU_AFTER[e]:
+                activate(e)
+            if chunk == CHUNKS - 1:
+                raw2 = raws.tile([P, E, PACK, N], F32, name="raw")
+                for d in range(E - 1):
+                    down[d] = down_weights(d, raw2[:, d, :, :])
+                    y = second_layer(d, slice(0, C))
+                    early = keep.tile([P, RANKS, HALF], F32, name="early%d" % d)
+                    nc.scalar.copy(out=early[:], in_=y[:].rearrange("p (m u) -> p m u", m=RANKS))
+                    nc.sync.dma_start(out=by_rank[:, :, d, :], in_=early[:])
+            if place == 2 * PASSES - 1:
+                gate(e)
+
+        down[E - 1] = down_weights(E - 1, raw2[:, E - 1, :, :])
         for m in range(RANKS):
             y = second_layer(E - 1, slice(m * HALF, (m + 1) * HALF))
             late = keep.tile([P, HALF], F32, name="late%d" % m)
-            if m == 0:
+            if m == 1:
                 nc.scalar.copy(out=late[:], in_=y[:, :HALF])
             else:
                 nc.vector.tensor_copy(out=late[:], in_=y[:, :HALF])
             nc.sync.dma_start(out=by_rank[:, m, E - 1, :], in_=late[:])
-        for e in range(E - 1):
-            y = second_layer(e, slice(0, C))
-            nc.scalar.copy(out=early[:, :, e, :], in_=y[:].rearrange("p (m u) -> p m u", m=RANKS))
-        nc.sync.dma_start(out=by_rank[:, :, : E - 1, :], in_=early[:])

@@ -28,7 +28,7 @@ GELU_AFTER = (1, 0, 0, 1)
 SPLIT_SHARE = (48, 44)
 CHUNKS = 2 * E * PASSES
 GROUPS = [(c,) for c in range(CHUNKS)]
-VECTOR_SHARE = [48] * 6 + [72] * 12 + [56, 56, 16, 56, 72]
+VECTOR_SHARE = [32] * 6 + [56] * 12 + [48, 48, 16, 48, 64]
 LOAD_CUTS = [(), (3,), (3,), (3,), (2, 1), (2, 1), (1, 1, 1), (1, 1)]
 
 

@@ -21,109 +21,97 @@ PACK = 4
 K_PASS = P * PACK
 PASSES = K // K_PASS
 HALF = C // RANKS
-GATHER = C
-GATHERS = {0: [(0, 0), (3, 0)], 1: [(1, 0)], 2: [(2, 0)], 3: [(0, 1), (3, 1)], 4: [(1, 1)], 5: [(2, 1)],
-           7: [(0, 2), (3, 2)], 8: [(1, 2)], 9: [(2, 2)], 13: [(0, 3), (3, 3)], 14: [(1, 3)], 15: [(2, 3)]}
-GELU_AFTER = (1, 0, 0, 1)
-SPLIT_SHARE = (48, 44)
-CHUNKS = 2 * E * PASSES
-GROUPS = [(c,) for c in range(CHUNKS)]
-VECTOR_SHARE = [32] * 6 + [56] * 12 + [48, 48, 16, 48, 64]
-LOAD_CUTS = [(), (3,), (3,), (3,), (2, 1), (2, 1), (1, 1, 1), (1, 1)]
+GATHER = 2 * C
+MATRICES = 2 * E
+CHUNKS = MATRICES * PASSES
+WHOLE = 5
+GATE_SHARE = 40
+UP_SHARE = 80
 
 
 def tile_moe_pke_glu_gelu_kernel(tc, x_words, x_scales, w1, w3, w2, offs, out):
     nc = tc.nc
     with ExitStack() as ctx:
         keep = ctx.enter_context(tc.tile_pool(name="keep", bufs=1))
-        raws = ctx.enter_context(tc.tile_pool(name="raws", bufs=4))
+        raws = ctx.enter_context(tc.tile_pool(name="raws", bufs=5))
         ring = ctx.enter_context(tc.tile_pool(name="ring", bufs=4))
         psum = ctx.enter_context(tc.psum_pool(name="psum", bufs=1))
         psum_y = ctx.enter_context(tc.psum_pool(name="psum_y", bufs=4))
 
-        def load_passes(raw, w, e, o0, count):
-            rows = w[e].rearrange("(o p j) c -> p o (j c)", o=PASSES, j=PACK)
-            nc.sync.dma_start(out=raw[:, o0 : o0 + count, :], in_=rows[:, o0 : o0 + count, :])
-
-        def load_words(o):
-            words = keep.tile([P, T], I32, name="token_words%d" % o, align_bytes=64)
-            nc.sync.dma_start(out=words[:], in_=x_words[o].rearrange("p t r -> p (t r)").bitcast(I32))
-            return words
-
+        words_hbm = x_words.rearrange("o p t r -> p o (t r)").bitcast(I32)
+        first_words = keep.tile([P, T], I32, name="first_words", align_bytes=64)
+        nc.sync.dma_start(out=first_words[:], in_=words_hbm[:, 0, :])
         offsets = keep.tile([P, E * C // 16], U16, name="offsets")
         nc.sync.dma_start(offsets[:], offs)
-        first_raw = raws.tile([P, PASSES, PACK * H], F32, name="raw")
-        load_passes(first_raw, w1, 0, 0, 1)
-        token_words = [load_words(0)]
-        load_passes(first_raw, w1, 0, 1, 1)
+        later_words = keep.tile([P, PASSES - 1, T], I32, name="later_words", align_bytes=64)
+        nc.sync.dma_start(out=later_words[:], in_=words_hbm[:, 1:, :])
+        token_words = [first_words[:]] + [later_words[:, o, :] for o in range(PASSES - 1)]
 
         token_scales = keep.tile([P, T], U8, name="token_scales", align_bytes=64)
         nc.vector.memset(token_scales[:].bitcast(I32), 0)
-        landed_scales = keep.tile([P, T // 4], I32, name="landed_scales")
-        for q in range(4):
-            live = slice(32 * q, 32 * q + 4 * PASSES)
-            nc.sync.dma_start(out=landed_scales[live, :], in_=x_scales[:, 4 * q : 4 * q + 4, :].bitcast(I32))
-            nc.vector.tensor_copy(out=token_scales[live, :].bitcast(I32), in_=landed_scales[live, :])
-        token_words.append(load_words(1))
-        load_passes(first_raw, w1, 0, 2, 1)
-        token_words.append(load_words(2))
-
         slot_words = [keep.tile([P, E * C], U32, name="slot_words%d" % o, align_bytes=64) for o in range(PASSES)]
         slot_scales = keep.tile([P, E * C], U8, name="slot_scales", align_bytes=64)
 
-        def gather(gathered, window, piece):
-            picks = offsets[:, piece * GATHER // 16 : (piece + 1) * GATHER // 16]
-            nc.vector.tensor_copy(gathered[:, piece * GATHER : (piece + 1) * GATHER], window.indirect(picks))
+        def gather(gathered, window):
+            for piece in range(E * C // GATHER):
+                picks = offsets[:, piece * GATHER // 16 : (piece + 1) * GATHER // 16]
+                nc.vector.tensor_copy(gathered[:, piece * GATHER : (piece + 1) * GATHER], window.indirect(picks))
 
-        raw_tiles = {0: first_raw}
-        banks = {}
+        def load(index):
+            raw = raws.tile([P, PASSES, PACK * H], F32, name="raw")
+            rows = (w1, w3)[index % 2][index // 2].rearrange("(o p j) c -> p o (j c)", o=PASSES, j=PACK)
+            if index < WHOLE:
+                cuts = [(0, PASSES)]
+            elif index == WHOLE:
+                cuts = [(0, PASSES - 1), (PASSES - 1, PASSES)]
+            else:
+                cuts = [(o, o + 1) for o in range(PASSES)]
+            if index == MATRICES - 1:
+                cuts = cuts[:-1]
+            for o0, o1 in cuts:
+                nc.sync.dma_start(out=raw[:, o0:o1, :], in_=rows[:, o0:o1, :])
+            if index == MATRICES - 1:
+                landing = raw[:, PASSES - 1, :].rearrange("p (j c) -> p j c", j=PACK)
+                last = rows[:, PASSES - 1, :].rearrange("p (j c) -> p j c", j=PACK)
+                for half in range(2):
+                    cols = slice(half * H // 2, (half + 1) * H // 2)
+                    nc.sync.dma_start(out=landing[:, :, cols], in_=last[:, :, cols])
+            return raw
 
-        def cast(chunk, grouped, codes, scales):
-            index, o = divmod(chunk, PASSES)
-            if index not in raw_tiles:
-                raw_tiles[index] = raws.tile([P, PASSES, PACK * H], F32, name="raw")
-                o0 = 0
-                for count in LOAD_CUTS[index]:
-                    load_passes(raw_tiles[index], (w1, w3)[index % 2], index // 2, o0, count)
-                    o0 += count
-            src = raw_tiles[index][:, o, :].rearrange("p (j m t) -> p m j t", j=PACK, t=PACK)
+        first_raw = load(0)
+        for q in range(4):
+            live = slice(32 * q, 32 * q + 4 * PASSES)
+            nc.sync.dma_start(out=token_scales[live, :].bitcast(I32), in_=x_scales[:, 4 * q : 4 * q + 4, :].bitcast(I32))
+
+        for o in range(PASSES):
+            gather(slot_words[o], token_words[o].bitcast(U32))
+        gather(slot_scales, token_scales[:])
+
+        def cast(src, dst, m0, cut, m1):
+            nc.scalar.copy(out=dst[:, cut:m1, :, :], in_=src[:, cut:m1, :, :])
+            nc.vector.tensor_copy(out=dst[:, m0:cut, :, :], in_=src[:, m0:cut, :, :])
+
+        def quantise(raw_pass, grouped, codes, scales, share, in_halves):
+            src = raw_pass.rearrange("p (j m t) -> p m j t", j=PACK, t=PACK)
             dst = grouped.rearrange("p (t m j) -> p m j t", t=PACK, j=PACK)
-            if chunk < CHUNKS - 1:
-                cut = VECTOR_SHARE[chunk]
-                nc.scalar.copy(out=dst[:, cut:, :, :], in_=src[:, cut:, :, :])
-                nc.vector.tensor_copy(out=dst[:, :cut, :, :], in_=src[:, :cut, :, :])
+            if not in_halves:
+                cast(src, dst, 0, share, P)
                 nc.vector.quantize_mx(out=codes.bitcast(FP8X4), scales=scales, in_=grouped)
                 return
-            landing = raw_tiles[index][:, o, :].rearrange("p (j c) -> p j c", j=PACK)
-            rows = w3[E - 1, K - K_PASS :, :].rearrange("(p j) c -> p j c", j=PACK)
-            for half in range(2):
-                c0, c1 = half * H // 2, (half + 1) * H // 2
-                nc.sync.dma_start(out=landing[:, :, c0:c1], in_=rows[:, :, c0:c1])
-            for half in range(2):
-                m0, m1 = half * P // 2, (half + 1) * P // 2
-                cut = m0 + SPLIT_SHARE[half]
-                nc.scalar.copy(out=dst[:, cut:m1, :, :], in_=src[:, cut:m1, :, :])
-                nc.vector.tensor_copy(out=dst[:, m0:cut, :, :], in_=src[:, m0:cut, :, :])
-                for t in range(PACK):
-                    w0, w1_ = t * P + m0, t * P + m1
-                    nc.vector.quantize_mx(
-                        out=codes[:, w0:w1_].bitcast(FP8X4),
-                        scales=scales[:, w0:w1_],
-                        in_=grouped[:, PACK * w0 : PACK * w1_],
-                    )
+            nc.scalar.copy(out=dst[:, : P // 2, :, :], in_=src[:, : P // 2, :, :])
+            cast(src, dst, P // 2, (P + share) // 2, P)
+            for t in range(PACK):
+                c0, c1 = t * P, (t + 1) * P
+                nc.vector.quantize_mx(
+                    out=codes[:, c0:c1].bitcast(FP8X4), scales=scales[:, c0:c1], in_=grouped[:, PACK * c0 : PACK * c1]
+                )
 
-        def multiply(chunk, codes, scales):
-            index, o = divmod(chunk, PASSES)
-            e = index // 2
-            if o == 0:
-                tag = ("gate", "up")[index % 2]
-                banks[index] = [psum.tile([P, PACK, HALF], F32, name="%s%d" % (tag, m)) for m in range(RANKS)]
-            order = [(m, t) for m in range(RANKS) for t in range(PACK)]
-            for m, t in order:
+        def multiply(banks, e, o, codes, scales):
+            for m in range(RANKS):
                 cols = slice(e * C + m * HALF, e * C + (m + 1) * HALF)
-                if True:
+                for t in range(PACK):
                     nc.tensor.matmul_mx(
-                        out=banks[index][m][:, t, :],
+                        out=banks[m][:, t, :],
                         lhsT=codes[:, t * P : (t + 1) * P].bitcast(FP8X4),
                         lhsT_scale=scales[:, t * P : (t + 1) * P],
                         rhs=slot_words[o][:, cols].bitcast(FP8X4),
@@ -132,99 +120,104 @@ def tile_moe_pke_glu_gelu_kernel(tc, x_words, x_scales, w1, w3, w2, offs, out):
                         stop=(o == PASSES - 1 and t == PACK - 1),
                     )
 
-        by_rank = out.rearrange("n (m e u) -> n m e u", m=RANKS, e=E)
+        def activate(banks, spent):
+            acts = []
+            for m in range(RANKS):
+                act = spent[:, m * H : (m + 1) * H].rearrange("p (u t) -> p u t", t=PACK)
+                nc.scalar.activation(out=act, in_=banks[m][:].rearrange("p t u -> p u t"), func=GELU)
+                acts.append(act)
+            return acts
 
-        def down_weights(e, raw2):
-            nc.sync.dma_start(out=raw2, in_=w2[e].rearrange("(p j) n -> p j n", j=PACK))
-            grouped2 = keep.tile([P, N * PACK], BF16, name="grouped2_%d" % e, align_bytes=64)
-            copy = nc.vector.tensor_copy if e == 1 else nc.scalar.copy
-            copy(
-                out=grouped2[:].rearrange("p (c i j) -> p c j i", i=4, j=PACK),
-                in_=raw2.rearrange("p j (c i) -> p c j i", i=4),
+        def gate(banks, acts, h):
+            for m in range(RANKS):
+                nc.vector.tensor_tensor(
+                    out=h[:, m * H : (m + 1) * H].rearrange("p (u t) -> p u t", t=PACK),
+                    in0=banks[m][:].rearrange("p t u -> p u t"),
+                    in1=acts[m],
+                    op=MULT,
+                )
+
+        def quantise_hidden(e, h):
+            h_codes = keep.tile([P, C], U32, name="h_codes%d" % e, align_bytes=64)
+            h_scales = keep.tile([P, C], U8, name="h_scales%d" % e, align_bytes=64)
+            width = HALF if e == E - 1 else C
+            for c0 in range(0, C, width):
+                cols = slice(c0, c0 + width)
+                nc.vector.quantize_mx(
+                    out=h_codes[:, cols].bitcast(FP8X4), scales=h_scales[:, cols], in_=h[:, PACK * c0 : PACK * (c0 + width)]
+                )
+            return h_codes, h_scales
+
+        def down_weights(e0, e1, raw2):
+            count = e1 - e0
+            grouped2 = keep.tile([P, count, N * PACK], BF16, name="grouped2_%d" % e0, align_bytes=64)
+            for d in range(count):
+                nc.scalar.copy(
+                    out=grouped2[:, d, :].rearrange("p (c i j) -> p c j i", i=4, j=PACK),
+                    in_=raw2[:, e0 + d, :].rearrange("p (j c i) -> p c j i", i=4, j=PACK),
+                )
+            codes2 = keep.tile([P, count * N], U32, name="codes2_%d" % e0, align_bytes=64)
+            scales2 = keep.tile([P, count * N], U8, name="scales2_%d" % e0, align_bytes=64)
+            nc.vector.quantize_mx(
+                out=codes2[:].bitcast(FP8X4), scales=scales2[:], in_=grouped2[:].rearrange("p d x -> p (d x)")
             )
-            codes2 = keep.tile([P, N], U32, name="codes2_%d" % e, align_bytes=64)
-            scales2 = keep.tile([P, N], U8, name="scales2_%d" % e, align_bytes=64)
-            nc.vector.quantize_mx(out=codes2[:].bitcast(FP8X4), scales=scales2[:], in_=grouped2[:])
-            return codes2, scales2
+            return [(codes2[:, d * N : (d + 1) * N], scales2[:, d * N : (d + 1) * N]) for d in range(count)]
 
-        def second_layer(e, cols):
-            codes2, scales2 = down[e]
-            h_codes, h_scales = hidden[e]
+        def second_layer(e, c0, c1):
             y = psum_y.tile([P, C], F32, name="y")
-            width = cols.stop - cols.start
             nc.tensor.matmul_mx(
-                out=y[:, :width],
-                lhsT=codes2[:].bitcast(FP8X4),
-                lhsT_scale=scales2[:],
-                rhs=h_codes[:, cols].bitcast(FP8X4),
-                rhs_scale=h_scales[:, cols],
+                out=y[:, : c1 - c0],
+                lhsT=down[e][0].bitcast(FP8X4),
+                lhsT_scale=down[e][1],
+                rhs=hidden[e][0][:, c0:c1].bitcast(FP8X4),
+                rhs_scale=hidden[e][1][:, c0:c1],
                 start=True,
                 stop=True,
             )
-            return y
+            return y[:, : c1 - c0]
 
-        down = {}
         hidden = []
-        acts = {}
-
-        def activate(e):
-            acts[e] = []
-            for m in range(RANKS):
-                act = raw_tiles[2 * e + 1][:, GELU_AFTER[e], m * H : (m + 1) * H].rearrange("p (u t) -> p u t", t=PACK)
-                nc.scalar.activation(out=act, in_=banks[2 * e][m][:].rearrange("p t u -> p u t"), func=GELU)
-                acts[e].append(act)
-
-        def gate(e):
-            h = ring.tile([P, C, PACK], BF16, name="h", align_bytes=64)
-            for m in range(RANKS):
-                nc.vector.tensor_tensor(
-                    out=h[:, m * HALF : (m + 1) * HALF, :],
-                    in0=banks[2 * e + 1][m][:].rearrange("p t u -> p u t"),
-                    in1=acts[e][m],
-                    op=MULT,
-                )
-            h_codes = keep.tile([P, C], U32, name="h_codes%d" % e, align_bytes=64)
-            h_scales = keep.tile([P, C], U8, name="h_scales%d" % e, align_bytes=64)
-            for m in range(RANKS):
-                cols = slice(m * HALF, (m + 1) * HALF)
-                nc.vector.quantize_mx(
-                    out=h_codes[:, cols].bitcast(FP8X4),
-                    scales=h_scales[:, cols],
-                    in_=h[:, cols, :].rearrange("p u t -> p (u t)"),
-                )
-            hidden.append((h_codes, h_scales))
-
-        for chunk in range(CHUNKS):
-            grouped = ring.tile([P, PACK * H], BF16, name="grouped", align_bytes=64)
-            codes = ring.tile([P, H], U32, name="codes", align_bytes=64)
-            scales = ring.tile([P, H], U8, name="scales", align_bytes=64)
-            cast(chunk, grouped[:], codes[:], scales[:])
-            for kind, e in GATHERS.get(chunk, []):
-                if kind < PASSES:
-                    gather(slot_words[kind], token_words[kind][:].bitcast(U32), e)
-                else:
-                    gather(slot_scales, token_scales[:], e)
-            multiply(chunk, codes[:], scales[:])
-            e, place = divmod(chunk, 2 * PASSES)
-            if place == PASSES + GELU_AFTER[e]:
-                activate(e)
-            if chunk == CHUNKS - 1:
-                raw2 = raws.tile([P, E, PACK, N], F32, name="raw")
-                for d in range(E - 1):
-                    down[d] = down_weights(d, raw2[:, d, :, :])
-                    y = second_layer(d, slice(0, C))
-                    early = keep.tile([P, RANKS, HALF], F32, name="early%d" % d)
-                    nc.scalar.copy(out=early[:], in_=y[:].rearrange("p (m u) -> p m u", m=RANKS))
-                    nc.sync.dma_start(out=by_rank[:, :, d, :], in_=early[:])
-            if place == 2 * PASSES - 1:
-                gate(e)
-
-        down[E - 1] = down_weights(E - 1, raw2[:, E - 1, :, :])
-        for m in range(RANKS):
-            y = second_layer(E - 1, slice(m * HALF, (m + 1) * HALF))
-            late = keep.tile([P, HALF], F32, name="late%d" % m)
-            if m == 1:
-                nc.scalar.copy(out=late[:], in_=y[:, :HALF])
+        for index in range(MATRICES):
+            e, is_up = divmod(index, 2)
+            raw = load(index) if index else first_raw
+            banks = [psum.tile([P, PACK, HALF], F32, name="%s%d" % (("gate", "up")[is_up], m)) for m in range(RANKS)]
+            for o in range(PASSES):
+                grouped = ring.tile([P, PACK * H], BF16, name="grouped", align_bytes=64)
+                codes = ring.tile([P, H], U32, name="codes", align_bytes=64)
+                scales = ring.tile([P, H], U8, name="scales", align_bytes=64)
+                is_last = index == MATRICES - 1
+                share = UP_SHARE if is_up else GATE_SHARE
+                quantise(raw[:, o, :], grouped[:], codes[:], scales[:], share, is_last and o == PASSES - 1)
+                multiply(banks, e, o, codes[:], scales[:])
+                if o == 0 and is_up:
+                    acts = activate(gate_banks, raw[:, 0, :])
+                if o == 0 and not is_up and e > 0:
+                    gate(up_banks, acts, grouped[:])
+                    hidden.append(quantise_hidden(e - 1, grouped[:]))
+            if is_up:
+                up_banks = banks
             else:
-                nc.vector.tensor_copy(out=late[:], in_=y[:, :HALF])
+                gate_banks = banks
+
+        raw2 = raws.tile([P, E, PACK * N], F32, name="raw")
+        for e in range(E):
+            nc.sync.dma_start(out=raw2[:, e, :], in_=w2[e].rearrange("(p j) n -> p (j n)", j=PACK))
+        down = down_weights(0, 1, raw2) + down_weights(1, 2, raw2)
+        last_h = ring.tile([P, PACK * H], BF16, name="grouped", align_bytes=64)
+        gate(up_banks, acts, last_h[:])
+        down = down + down_weights(2, E, raw2)
+        hidden.append(quantise_hidden(E - 1, last_h[:]))
+
+        by_rank = out.rearrange("n (m e u) -> n m e u", m=RANKS, e=E)
+        early = raw2[:, E - 1, :].rearrange("p (m e u) -> p m e u", m=RANKS, e=2)
+        for e in range(2):
+            nc.scalar.copy(out=early[:, :, e, :], in_=second_layer(e, 0, C).rearrange("p (m u) -> p m u", m=RANKS))
+        nc.sync.dma_start(out=by_rank[:, :, :2, :], in_=early)
+        third = keep.tile([P, RANKS, HALF], F32, name="third")
+        nc.scalar.copy(out=third[:], in_=second_layer(E - 2, 0, C).rearrange("p (m u) -> p m u", m=RANKS))
+        nc.sync.dma_start(out=by_rank[:, :, E - 2, :], in_=third[:])
+        for m in range(RANKS):
+            late = keep.tile([P, HALF], F32, name="late%d" % m)
+            copy = nc.scalar.copy if m == 0 else nc.vector.tensor_copy
+            copy(out=late[:], in_=second_layer(E - 1, m * HALF, (m + 1) * HALF))
             nc.sync.dma_start(out=by_rank[:, m, E - 1, :], in_=late[:])

@@ -21,7 +21,6 @@ PACK = 4
 K_PASS = P * PACK
 PASSES = K // K_PASS
 HALF = C // RANKS
-GATHER = 2 * C
 MATRICES = 2 * E
 CHUNKS = MATRICES * PASSES
 WHOLE = 5
@@ -38,28 +37,41 @@ def tile_moe_pke_glu_gelu_kernel(tc, x_words, x_scales, w1, w3, w2, offs, out):
         psum = ctx.enter_context(tc.psum_pool(name="psum", bufs=1))
         psum_y = ctx.enter_context(tc.psum_pool(name="psum_y", bufs=4))
 
+        def weight_rows(index):
+            return (w1, w3)[index % 2][index // 2].rearrange("(o p j) c -> p o (j c)", o=PASSES, j=PACK)
+
+        first_raw = raws.tile([P, PASSES, PACK * H], F32, name="raw")
+        nc.sync.dma_start(out=first_raw[:, 0, :], in_=weight_rows(0)[:, 0, :])
+        offsets = keep.tile([P, E * C // 16], U16, name="offsets")
+        nc.sync.dma_start(offsets[:], offs)
         words_hbm = x_words.rearrange("o p t r -> p o (t r)").bitcast(I32)
         first_words = keep.tile([P, T], I32, name="first_words", align_bytes=64)
         nc.sync.dma_start(out=first_words[:], in_=words_hbm[:, 0, :])
-        offsets = keep.tile([P, E * C // 16], U16, name="offsets")
-        nc.sync.dma_start(offsets[:], offs)
-        later_words = keep.tile([P, PASSES - 1, T], I32, name="later_words", align_bytes=64)
-        nc.sync.dma_start(out=later_words[:], in_=words_hbm[:, 1:, :])
-        token_words = [first_words[:]] + [later_words[:, o, :] for o in range(PASSES - 1)]
+        nc.sync.dma_start(out=first_raw[:, 1, :], in_=weight_rows(0)[:, 1, :])
 
         token_scales = keep.tile([P, T], U8, name="token_scales", align_bytes=64)
         nc.vector.memset(token_scales[:].bitcast(I32), 0)
+        landed_scales = keep.tile([P, T // 4], I32, name="landed_scales")
+        for q in range(4):
+            live = slice(32 * q, 32 * q + 4 * PASSES)
+            nc.sync.dma_start(out=landed_scales[live, :], in_=x_scales[:, 4 * q : 4 * q + 4, :].bitcast(I32))
+            nc.vector.tensor_copy(out=token_scales[live, :].bitcast(I32), in_=landed_scales[live, :])
+
+        later_words = keep.tile([P, PASSES - 1, T], I32, name="later_words", align_bytes=64)
+        nc.sync.dma_start(out=later_words[:], in_=words_hbm[:, 1:, :])
+        nc.sync.dma_start(out=first_raw[:, 2, :], in_=weight_rows(0)[:, 2, :])
+        token_words = [first_words[:]] + [later_words[:, o, :] for o in range(PASSES - 1)]
+
         slot_words = [keep.tile([P, E * C], U32, name="slot_words%d" % o, align_bytes=64) for o in range(PASSES)]
         slot_scales = keep.tile([P, E * C], U8, name="slot_scales", align_bytes=64)
 
-        def gather(gathered, window):
-            for piece in range(E * C // GATHER):
-                picks = offsets[:, piece * GATHER // 16 : (piece + 1) * GATHER // 16]
-                nc.vector.tensor_copy(gathered[:, piece * GATHER : (piece + 1) * GATHER], window.indirect(picks))
+        def gather(gathered, window, e):
+            picks = offsets[:, e * C // 16 : (e + 1) * C // 16]
+            nc.vector.tensor_copy(gathered[:, e * C : (e + 1) * C], window.indirect(picks))
 
         def load(index):
             raw = raws.tile([P, PASSES, PACK * H], F32, name="raw")
-            rows = (w1, w3)[index % 2][index // 2].rearrange("(o p j) c -> p o (j c)", o=PASSES, j=PACK)
+            rows = weight_rows(index)
             if index < WHOLE:
                 cuts = [(0, PASSES)]
             elif index == WHOLE:
@@ -77,15 +89,6 @@ def tile_moe_pke_glu_gelu_kernel(tc, x_words, x_scales, w1, w3, w2, offs, out):
                     cols = slice(half * H // 2, (half + 1) * H // 2)
                     nc.sync.dma_start(out=landing[:, :, cols], in_=last[:, :, cols])
             return raw
-
-        first_raw = load(0)
-        for q in range(4):
-            live = slice(32 * q, 32 * q + 4 * PASSES)
-            nc.sync.dma_start(out=token_scales[live, :].bitcast(I32), in_=x_scales[:, 4 * q : 4 * q + 4, :].bitcast(I32))
-
-        for o in range(PASSES):
-            gather(slot_words[o], token_words[o].bitcast(U32))
-        gather(slot_scales, token_scales[:])
 
         def cast(src, dst, m0, cut, m1):
             nc.scalar.copy(out=dst[:, cut:m1, :, :], in_=src[:, cut:m1, :, :])
@@ -107,9 +110,9 @@ def tile_moe_pke_glu_gelu_kernel(tc, x_words, x_scales, w1, w3, w2, offs, out):
                 )
 
         def multiply(banks, e, o, codes, scales):
-            for m in range(RANKS):
-                cols = slice(e * C + m * HALF, e * C + (m + 1) * HALF)
-                for t in range(PACK):
+            for t in range(PACK):
+                for m in range(RANKS):
+                    cols = slice(e * C + m * HALF, e * C + (m + 1) * HALF)
                     nc.tensor.matmul_mx(
                         out=banks[m][:, t, :],
                         lhsT=codes[:, t * P : (t + 1) * P].bitcast(FP8X4),
@@ -128,49 +131,36 @@ def tile_moe_pke_glu_gelu_kernel(tc, x_words, x_scales, w1, w3, w2, offs, out):
                 acts.append(act)
             return acts
 
-        def gate(banks, acts, h):
+        def gate(banks, acts, outs):
             for m in range(RANKS):
                 nc.vector.tensor_tensor(
-                    out=h[:, m * H : (m + 1) * H].rearrange("p (u t) -> p u t", t=PACK),
+                    out=outs[m].rearrange("p (u t) -> p u t", t=PACK),
                     in0=banks[m][:].rearrange("p t u -> p u t"),
                     in1=acts[m],
                     op=MULT,
                 )
 
-        def quantise_hidden(e, h):
-            h_codes = keep.tile([P, C], U32, name="h_codes%d" % e, align_bytes=64)
-            h_scales = keep.tile([P, C], U8, name="h_scales%d" % e, align_bytes=64)
-            width = HALF if e == E - 1 else C
-            for c0 in range(0, C, width):
-                cols = slice(c0, c0 + width)
-                nc.vector.quantize_mx(
-                    out=h_codes[:, cols].bitcast(FP8X4), scales=h_scales[:, cols], in_=h[:, PACK * c0 : PACK * (c0 + width)]
-                )
-            return h_codes, h_scales
+        def quantise_kept(values, name):
+            width = values.shape[1] // PACK
+            codes = keep.tile([P, width], U32, name=name + "_codes", align_bytes=64)
+            scales = keep.tile([P, width], U8, name=name + "_scales", align_bytes=64)
+            nc.vector.quantize_mx(out=codes[:].bitcast(FP8X4), scales=scales[:], in_=values)
+            return codes, scales
 
-        def down_weights(e0, e1, raw2):
-            count = e1 - e0
-            grouped2 = keep.tile([P, count, N * PACK], BF16, name="grouped2_%d" % e0, align_bytes=64)
-            for d in range(count):
-                nc.scalar.copy(
-                    out=grouped2[:, d, :].rearrange("p (c i j) -> p c j i", i=4, j=PACK),
-                    in_=raw2[:, e0 + d, :].rearrange("p (j c i) -> p c j i", i=4, j=PACK),
-                )
-            codes2 = keep.tile([P, count * N], U32, name="codes2_%d" % e0, align_bytes=64)
-            scales2 = keep.tile([P, count * N], U8, name="scales2_%d" % e0, align_bytes=64)
-            nc.vector.quantize_mx(
-                out=codes2[:].bitcast(FP8X4), scales=scales2[:], in_=grouped2[:].rearrange("p d x -> p (d x)")
+        def cast_down(grouped2, raw_rows):
+            nc.scalar.copy(
+                out=grouped2.rearrange("p (c i j) -> p c j i", i=4, j=PACK),
+                in_=raw_rows.rearrange("p (j c i) -> p c j i", i=4, j=PACK),
             )
-            return [(codes2[:, d * N : (d + 1) * N], scales2[:, d * N : (d + 1) * N]) for d in range(count)]
 
-        def second_layer(e, c0, c1):
+        def second_layer(weights, w0, slots, c0, c1):
             y = psum_y.tile([P, C], F32, name="y")
             nc.tensor.matmul_mx(
                 out=y[:, : c1 - c0],
-                lhsT=down[e][0].bitcast(FP8X4),
-                lhsT_scale=down[e][1],
-                rhs=hidden[e][0][:, c0:c1].bitcast(FP8X4),
-                rhs_scale=hidden[e][1][:, c0:c1],
+                lhsT=weights[0][:, w0 : w0 + N].bitcast(FP8X4),
+                lhsT_scale=weights[1][:, w0 : w0 + N],
+                rhs=slots[0][:, c0:c1].bitcast(FP8X4),
+                rhs_scale=slots[1][:, c0:c1],
                 start=True,
                 stop=True,
             )
@@ -188,12 +178,16 @@ def tile_moe_pke_glu_gelu_kernel(tc, x_words, x_scales, w1, w3, w2, offs, out):
                 is_last = index == MATRICES - 1
                 share = UP_SHARE if is_up else GATE_SHARE
                 quantise(raw[:, o, :], grouped[:], codes[:], scales[:], share, is_last and o == PASSES - 1)
+                if index == 0 or (is_up and not is_last):
+                    gather(slot_words[o], token_words[o].bitcast(U32), e + is_up)
+                    if o == 0:
+                        gather(slot_scales, token_scales[:], e + is_up)
                 multiply(banks, e, o, codes[:], scales[:])
                 if o == 0 and is_up:
                     acts = activate(gate_banks, raw[:, 0, :])
                 if o == 0 and not is_up and e > 0:
-                    gate(up_banks, acts, grouped[:])
-                    hidden.append(quantise_hidden(e - 1, grouped[:]))
+                    gate(up_banks, acts, [grouped[:, m * H : (m + 1) * H] for m in range(RANKS)])
+                    hidden.append(quantise_kept(grouped[:, : RANKS * H], "hidden%d" % e))
             if is_up:
                 up_banks = banks
             else:
@@ -202,22 +196,29 @@ def tile_moe_pke_glu_gelu_kernel(tc, x_words, x_scales, w1, w3, w2, offs, out):
         raw2 = raws.tile([P, E, PACK * N], F32, name="raw")
         for e in range(E):
             nc.sync.dma_start(out=raw2[:, e, :], in_=w2[e].rearrange("(p j) n -> p (j n)", j=PACK))
-        down = down_weights(0, 1, raw2) + down_weights(1, 2, raw2)
-        last_h = ring.tile([P, PACK * H], BF16, name="grouped", align_bytes=64)
-        gate(up_banks, acts, last_h[:])
-        down = down + down_weights(2, E, raw2)
-        hidden.append(quantise_hidden(E - 1, last_h[:]))
+        down = []
+        for e in range(E - RANKS):
+            grouped2 = keep.tile([P, PACK * N], BF16, name="grouped2_%d" % e, align_bytes=64)
+            cast_down(grouped2[:], raw2[:, e, :])
+            down.append(quantise_kept(grouped2[:], "down%d" % e))
+        joint = [keep.tile([P, H + PACK * N], BF16, name="joint%d" % m, align_bytes=64) for m in range(RANKS)]
+        gate(up_banks, acts, [joint[m][:, :H] for m in range(RANKS)])
+        for m in range(RANKS):
+            cast_down(joint[m][:, H:], raw2[:, E - RANKS + m, :])
+        last = [quantise_kept(joint[m][:], "last%d" % m) for m in range(RANKS)]
 
         by_rank = out.rearrange("n (m e u) -> n m e u", m=RANKS, e=E)
         early = raw2[:, E - 1, :].rearrange("p (m e u) -> p m e u", m=RANKS, e=2)
-        for e in range(2):
-            nc.scalar.copy(out=early[:, :, e, :], in_=second_layer(e, 0, C).rearrange("p (m u) -> p m u", m=RANKS))
+        for e in range(E - RANKS):
+            y = second_layer(down[e], 0, hidden[e], 0, C)
+            nc.scalar.copy(out=early[:, :, e, :], in_=y.rearrange("p (m u) -> p m u", m=RANKS))
         nc.sync.dma_start(out=by_rank[:, :, :2, :], in_=early)
         third = keep.tile([P, RANKS, HALF], F32, name="third")
-        nc.scalar.copy(out=third[:], in_=second_layer(E - 2, 0, C).rearrange("p (m u) -> p m u", m=RANKS))
+        y = second_layer(last[0], HALF, hidden[E - 2], 0, C)
+        nc.scalar.copy(out=third[:], in_=y.rearrange("p (m u) -> p m u", m=RANKS))
         nc.sync.dma_start(out=by_rank[:, :, E - 2, :], in_=third[:])
         for m in range(RANKS):
             late = keep.tile([P, HALF], F32, name="late%d" % m)
             copy = nc.scalar.copy if m == 0 else nc.vector.tensor_copy
-            copy(out=late[:], in_=second_layer(E - 1, m * HALF, (m + 1) * HALF))
+            copy(out=late[:], in_=second_layer(last[1], HALF, last[m], 0, HALF))
             nc.sync.dma_start(out=by_rank[:, m, E - 1, :], in_=late[:])

@@ -23,16 +23,17 @@ PASSES = K // K_PASS
 HALF = C // RANKS
 MATRICES = 2 * E
 CHUNKS = MATRICES * PASSES
-WHOLE = 5
-GATE_SHARE = 40
-UP_SHARE = 80
+WHOLE = 4
+GATE_SHARE = 32
+UP_SHARE = 64
+LAST_SHARE = 80
 
 
 def tile_moe_pke_glu_gelu_kernel(tc, x_words, x_scales, w1, w3, w2, offs, out):
     nc = tc.nc
     with ExitStack() as ctx:
         keep = ctx.enter_context(tc.tile_pool(name="keep", bufs=1))
-        raws = ctx.enter_context(tc.tile_pool(name="raws", bufs=5))
+        raws = ctx.enter_context(tc.tile_pool(name="raws", bufs=4))
         ring = ctx.enter_context(tc.tile_pool(name="ring", bufs=4))
         psum = ctx.enter_context(tc.psum_pool(name="psum", bufs=1))
         psum_y = ctx.enter_context(tc.psum_pool(name="psum_y", bufs=4))
@@ -70,25 +71,27 @@ def tile_moe_pke_glu_gelu_kernel(tc, x_words, x_scales, w1, w3, w2, offs, out):
             nc.vector.tensor_copy(gathered[:, e * C : (e + 1) * C], window.indirect(picks))
 
         def load(index):
-            raw = raws.tile([P, PASSES, PACK * H], F32, name="raw")
             rows = weight_rows(index)
+            if index == MATRICES - 1:
+                passes = [keep.tile([P, PACK * H], F32, name="last_pass%d" % o, align_bytes=64)[:] for o in range(PASSES)]
+                for o in range(PASSES - 1):
+                    nc.sync.dma_start(out=passes[o], in_=rows[:, o, :])
+                landing = passes[-1].rearrange("p (j c) -> p j c", j=PACK)
+                last = rows[:, PASSES - 1, :].rearrange("p (j c) -> p j c", j=PACK)
+                for half in range(2):
+                    cols = slice(half * H // 2, (half + 1) * H // 2)
+                    nc.sync.dma_start(out=landing[:, :, cols], in_=last[:, :, cols])
+                return passes
+            raw = raws.tile([P, PASSES, PACK * H], F32, name="raw")
             if index < WHOLE:
                 cuts = [(0, PASSES)]
             elif index == WHOLE:
                 cuts = [(0, PASSES - 1), (PASSES - 1, PASSES)]
             else:
                 cuts = [(o, o + 1) for o in range(PASSES)]
-            if index == MATRICES - 1:
-                cuts = cuts[:-1]
             for o0, o1 in cuts:
                 nc.sync.dma_start(out=raw[:, o0:o1, :], in_=rows[:, o0:o1, :])
-            if index == MATRICES - 1:
-                landing = raw[:, PASSES - 1, :].rearrange("p (j c) -> p j c", j=PACK)
-                last = rows[:, PASSES - 1, :].rearrange("p (j c) -> p j c", j=PACK)
-                for half in range(2):
-                    cols = slice(half * H // 2, (half + 1) * H // 2)
-                    nc.sync.dma_start(out=landing[:, :, cols], in_=last[:, :, cols])
-            return raw
+            return [raw[:, o, :] for o in range(PASSES)]
 
         def cast(src, dst, m0, cut, m1):
             nc.scalar.copy(out=dst[:, cut:m1, :, :], in_=src[:, cut:m1, :, :])
@@ -101,7 +104,7 @@ def tile_moe_pke_glu_gelu_kernel(tc, x_words, x_scales, w1, w3, w2, offs, out):
                 cast(src, dst, 0, share, P)
                 nc.vector.quantize_mx(out=codes.bitcast(FP8X4), scales=scales, in_=grouped)
                 return
-            nc.scalar.copy(out=dst[:, : P // 2, :, :], in_=src[:, : P // 2, :, :])
+            cast(src, dst, 0, share // 2, P // 2)
             cast(src, dst, P // 2, (P + share) // 2, P)
             for t in range(PACK):
                 c0, c1 = t * P, (t + 1) * P
@@ -110,9 +113,9 @@ def tile_moe_pke_glu_gelu_kernel(tc, x_words, x_scales, w1, w3, w2, offs, out):
                 )
 
         def multiply(banks, e, o, codes, scales):
-            for t in range(PACK):
-                for m in range(RANKS):
-                    cols = slice(e * C + m * HALF, e * C + (m + 1) * HALF)
+            for m in range(RANKS):
+                cols = slice(e * C + m * HALF, e * C + (m + 1) * HALF)
+                for t in range(PACK):
                     nc.tensor.matmul_mx(
                         out=banks[m][:, t, :],
                         lhsT=codes[:, t * P : (t + 1) * P].bitcast(FP8X4),
@@ -123,13 +126,10 @@ def tile_moe_pke_glu_gelu_kernel(tc, x_words, x_scales, w1, w3, w2, offs, out):
                         stop=(o == PASSES - 1 and t == PACK - 1),
                     )
 
-        def activate(banks, spent):
-            acts = []
-            for m in range(RANKS):
-                act = spent[:, m * H : (m + 1) * H].rearrange("p (u t) -> p u t", t=PACK)
-                nc.scalar.activation(out=act, in_=banks[m][:].rearrange("p t u -> p u t"), func=GELU)
-                acts.append(act)
-            return acts
+        def activate(bank, spent):
+            act = spent[:, :H].rearrange("p (u t) -> p u t", t=PACK)
+            nc.scalar.activation(out=act, in_=bank[:].rearrange("p t u -> p u t"), func=GELU)
+            return act
 
         def gate(banks, acts, outs):
             for m in range(RANKS):
@@ -140,9 +140,9 @@ def tile_moe_pke_glu_gelu_kernel(tc, x_words, x_scales, w1, w3, w2, offs, out):
                     op=MULT,
                 )
 
-        def quantise_kept(values, name):
+        def quantise_kept(values, name, codes_tag):
             width = values.shape[1] // PACK
-            codes = keep.tile([P, width], U32, name=name + "_codes", align_bytes=64)
+            codes = keep.tile([P, width], U32, name=codes_tag, align_bytes=64)
             scales = keep.tile([P, width], U8, name=name + "_scales", align_bytes=64)
             nc.vector.quantize_mx(out=codes[:].bitcast(FP8X4), scales=scales[:], in_=values)
             return codes, scales
@@ -167,27 +167,31 @@ def tile_moe_pke_glu_gelu_kernel(tc, x_words, x_scales, w1, w3, w2, offs, out):
             return y[:, : c1 - c0]
 
         hidden = []
+        acts = {}
         for index in range(MATRICES):
             e, is_up = divmod(index, 2)
-            raw = load(index) if index else first_raw
+            passes = load(index) if index else [first_raw[:, o, :] for o in range(PASSES)]
             banks = [psum.tile([P, PACK, HALF], F32, name="%s%d" % (("gate", "up")[is_up], m)) for m in range(RANKS)]
             for o in range(PASSES):
                 grouped = ring.tile([P, PACK * H], BF16, name="grouped", align_bytes=64)
                 codes = ring.tile([P, H], U32, name="codes", align_bytes=64)
                 scales = ring.tile([P, H], U8, name="scales", align_bytes=64)
                 is_last = index == MATRICES - 1
-                share = UP_SHARE if is_up else GATE_SHARE
-                quantise(raw[:, o, :], grouped[:], codes[:], scales[:], share, is_last and o == PASSES - 1)
+                if index * PASSES + o >= CHUNKS - 4:
+                    share = LAST_SHARE
+                else:
+                    share = UP_SHARE if is_up or o == PASSES - 1 else GATE_SHARE
+                quantise(passes[o], grouped[:], codes[:], scales[:], share, is_last and o == PASSES - 1)
                 if index == 0 or (is_up and not is_last):
                     gather(slot_words[o], token_words[o].bitcast(U32), e + is_up)
                     if o == 0:
                         gather(slot_scales, token_scales[:], e + is_up)
                 multiply(banks, e, o, codes[:], scales[:])
-                if o == 0 and is_up:
-                    acts = activate(gate_banks, raw[:, 0, :])
+                if is_up and o < RANKS:
+                    acts[o] = activate(gate_banks[o], passes[o])
                 if o == 0 and not is_up and e > 0:
                     gate(up_banks, acts, [grouped[:, m * H : (m + 1) * H] for m in range(RANKS)])
-                    hidden.append(quantise_kept(grouped[:, : RANKS * H], "hidden%d" % e))
+                    hidden.append(quantise_kept(grouped[:, : RANKS * H], "hidden%d" % e, "hidden%d" % e))
             if is_up:
                 up_banks = banks
             else:
@@ -196,29 +200,28 @@ def tile_moe_pke_glu_gelu_kernel(tc, x_words, x_scales, w1, w3, w2, offs, out):
         raw2 = raws.tile([P, E, PACK * N], F32, name="raw")
         for e in range(E):
             nc.sync.dma_start(out=raw2[:, e, :], in_=w2[e].rearrange("(p j) n -> p (j n)", j=PACK))
-        down = []
-        for e in range(E - RANKS):
-            grouped2 = keep.tile([P, PACK * N], BF16, name="grouped2_%d" % e, align_bytes=64)
-            cast_down(grouped2[:], raw2[:, e, :])
-            down.append(quantise_kept(grouped2[:], "down%d" % e))
-        joint = [keep.tile([P, H + PACK * N], BF16, name="joint%d" % m, align_bytes=64) for m in range(RANKS)]
-        gate(up_banks, acts, [joint[m][:, :H] for m in range(RANKS)])
-        for m in range(RANKS):
-            cast_down(joint[m][:, H:], raw2[:, E - RANKS + m, :])
-        last = [quantise_kept(joint[m][:], "last%d" % m) for m in range(RANKS)]
+        grouped2 = keep.tile([P, E, PACK * N], BF16, name="last_pass2", align_bytes=64)
+        for e in range(E):
+            cast_down(grouped2[:, e, :], raw2[:, e, :])
+        down0 = quantise_kept(grouped2[:, 0, :], "down0", "down0")
+        last_h = ring.tile([P, PACK * H], BF16, name="grouped", align_bytes=64)
+        gate(up_banks, acts, [last_h[:, m * H : (m + 1) * H] for m in range(RANKS)])
+        down1 = quantise_kept(grouped2[:, 1, :], "down1", "last_pass0")
+        down23 = quantise_kept(grouped2[:, 2:, :].rearrange("p e x -> p (e x)"), "down23", "last_pass1")
+        hidden.append(quantise_kept(last_h[:, : RANKS * H], "hidden_last", "hidden_last"))
 
         by_rank = out.rearrange("n (m e u) -> n m e u", m=RANKS, e=E)
-        early = raw2[:, E - 1, :].rearrange("p (m e u) -> p m e u", m=RANKS, e=2)
-        for e in range(E - RANKS):
-            y = second_layer(down[e], 0, hidden[e], 0, C)
-            nc.scalar.copy(out=early[:, :, e, :], in_=y.rearrange("p (m u) -> p m u", m=RANKS))
-        nc.sync.dma_start(out=by_rank[:, :, :2, :], in_=early)
+        early = raw2[:, E - 1, :].rearrange("p (e m u) -> p e m u", m=RANKS, e=2)
+        for e, down in enumerate((down0, down1)):
+            y = second_layer(down, 0, hidden[e], 0, C)
+            nc.scalar.copy(out=early[:, e, :, :], in_=y.rearrange("p (m u) -> p m u", m=RANKS))
+            nc.sync.dma_start(out=by_rank[:, :, e, :], in_=early[:, e, :, :])
         third = keep.tile([P, RANKS, HALF], F32, name="third")
-        y = second_layer(last[0], HALF, hidden[E - 2], 0, C)
+        y = second_layer(down23, 0, hidden[E - 2], 0, C)
         nc.scalar.copy(out=third[:], in_=y.rearrange("p (m u) -> p m u", m=RANKS))
         nc.sync.dma_start(out=by_rank[:, :, E - 2, :], in_=third[:])
         for m in range(RANKS):
             late = keep.tile([P, HALF], F32, name="late%d" % m)
             copy = nc.scalar.copy if m == 0 else nc.vector.tensor_copy
-            copy(out=late[:], in_=second_layer(last[1], HALF, last[m], 0, HALF))
+            copy(out=late[:], in_=second_layer(down23, N, hidden[E - 1], m * HALF, (m + 1) * HALF))
             nc.sync.dma_start(out=by_rank[:, m, E - 1, :], in_=late[:])

@@ -23,7 +23,7 @@ PASSES = K // K_PASS
 HALF = C // RANKS
 MATRICES = 2 * E
 CHUNKS = MATRICES * PASSES
-WHOLE = 4
+WHOLE = 2
 GATE_SHARE = 32
 UP_SHARE = 64
 LAST_SHARE = 80
@@ -104,7 +104,7 @@ def tile_moe_pke_glu_gelu_kernel(tc, x_words, x_scales, w1, w3, w2, offs, out):
                 cast(src, dst, 0, share, P)
                 nc.vector.quantize_mx(out=codes.bitcast(FP8X4), scales=scales, in_=grouped)
                 return
-            cast(src, dst, 0, share // 2, P // 2)
+            cast(src, dst, 0, UP_SHARE // 2, P // 2)
             cast(src, dst, P // 2, (P + share) // 2, P)
             for t in range(PACK):
                 c0, c1 = t * P, (t + 1) * P

@@ -27,6 +27,7 @@ WHOLE = 2
 GATE_SHARE = 32
 UP_SHARE = 64
 LAST_SHARE = 80
+LATE_SHARE = 40
 
 
 def tile_moe_pke_glu_gelu_kernel(tc, x_words, x_scales, w1, w3, w2, offs, out):
@@ -76,11 +77,9 @@ def tile_moe_pke_glu_gelu_kernel(tc, x_words, x_scales, w1, w3, w2, offs, out):
                 passes = [keep.tile([P, PACK * H], F32, name="last_pass%d" % o, align_bytes=64)[:] for o in range(PASSES)]
                 for o in range(PASSES - 1):
                     nc.sync.dma_start(out=passes[o], in_=rows[:, o, :])
-                landing = passes[-1].rearrange("p (j c) -> p j c", j=PACK)
-                last = rows[:, PASSES - 1, :].rearrange("p (j c) -> p j c", j=PACK)
                 for half in range(2):
-                    cols = slice(half * H // 2, (half + 1) * H // 2)
-                    nc.sync.dma_start(out=landing[:, :, cols], in_=last[:, :, cols])
+                    cols = slice(half * 2 * H, (half + 1) * 2 * H)
+                    nc.sync.dma_start(out=passes[-1][:, cols], in_=rows[:, PASSES - 1, cols])
                 return passes
             raw = raws.tile([P, PASSES, PACK * H], F32, name="raw")
             if index < WHOLE:
@@ -104,8 +103,10 @@ def tile_moe_pke_glu_gelu_kernel(tc, x_words, x_scales, w1, w3, w2, offs, out):
                 cast(src, dst, 0, share, P)
                 nc.vector.quantize_mx(out=codes.bitcast(FP8X4), scales=scales, in_=grouped)
                 return
-            cast(src, dst, 0, UP_SHARE // 2, P // 2)
-            cast(src, dst, P // 2, (P + share) // 2, P)
+            cast(src[:, :, :2, :], dst[:, :, :2, :], 0, share, P)
+            nc.scalar.copy(out=dst[:, LATE_SHARE:, 2:, 2:], in_=src[:, LATE_SHARE:, 2:, 2:])
+            nc.vector.tensor_copy(out=dst[:, :, 2:, :2], in_=src[:, :, 2:, :2])
+            nc.vector.tensor_copy(out=dst[:, :LATE_SHARE, 2:, 2:], in_=src[:, :LATE_SHARE, 2:, 2:])
             for t in range(PACK):
                 c0, c1 = t * P, (t + 1) * P
                 nc.vector.quantize_mx(
@@ -131,14 +132,10 @@ def tile_moe_pke_glu_gelu_kernel(tc, x_words, x_scales, w1, w3, w2, offs, out):
             nc.scalar.activation(out=act, in_=bank[:].rearrange("p t u -> p u t"), func=GELU)
             return act
 
-        def gate(banks, acts, outs):
-            for m in range(RANKS):
-                nc.vector.tensor_tensor(
-                    out=outs[m].rearrange("p (u t) -> p u t", t=PACK),
-                    in0=banks[m][:].rearrange("p t u -> p u t"),
-                    in1=acts[m],
-                    op=MULT,
-                )
+        def gate(bank, act, values):
+            nc.vector.tensor_tensor(
+                out=values.rearrange("p (u t) -> p u t", t=PACK), in0=bank[:].rearrange("p t u -> p u t"), in1=act, op=MULT
+            )
 
         def quantise_kept(values, name, codes_tag):
             width = values.shape[1] // PACK
@@ -147,24 +144,22 @@ def tile_moe_pke_glu_gelu_kernel(tc, x_words, x_scales, w1, w3, w2, offs, out):
             nc.vector.quantize_mx(out=codes[:].bitcast(FP8X4), scales=scales[:], in_=values)
             return codes, scales
 
-        def cast_down(grouped2, raw_rows):
-            nc.scalar.copy(
+        def cast_down(copy, grouped2, raw_rows):
+            copy(
                 out=grouped2.rearrange("p (c i j) -> p c j i", i=4, j=PACK),
                 in_=raw_rows.rearrange("p (j c i) -> p c j i", i=4, j=PACK),
             )
 
-        def second_layer(weights, w0, slots, c0, c1):
-            y = psum_y.tile([P, C], F32, name="y")
+        def second_layer(y, weights, slots):
             nc.tensor.matmul_mx(
-                out=y[:, : c1 - c0],
-                lhsT=weights[0][:, w0 : w0 + N].bitcast(FP8X4),
-                lhsT_scale=weights[1][:, w0 : w0 + N],
-                rhs=slots[0][:, c0:c1].bitcast(FP8X4),
-                rhs_scale=slots[1][:, c0:c1],
+                out=y,
+                lhsT=weights[0][:].bitcast(FP8X4),
+                lhsT_scale=weights[1][:],
+                rhs=slots[0][:].bitcast(FP8X4),
+                rhs_scale=slots[1][:],
                 start=True,
                 stop=True,
             )
-            return y[:, : c1 - c0]
 
         hidden = []
         acts = {}
@@ -190,7 +185,8 @@ def tile_moe_pke_glu_gelu_kernel(tc, x_words, x_scales, w1, w3, w2, offs, out):
                 if is_up and o < RANKS:
                     acts[o] = activate(gate_banks[o], passes[o])
                 if o == 0 and not is_up and e > 0:
-                    gate(up_banks, acts, [grouped[:, m * H : (m + 1) * H] for m in range(RANKS)])
+                    for m in range(RANKS):
+                        gate(up_banks[m], acts[m], grouped[:, m * H : (m + 1) * H])
                     hidden.append(quantise_kept(grouped[:, : RANKS * H], "hidden%d" % e, "hidden%d" % e))
             if is_up:
                 up_banks = banks
@@ -200,28 +196,28 @@ def tile_moe_pke_glu_gelu_kernel(tc, x_words, x_scales, w1, w3, w2, offs, out):
         raw2 = raws.tile([P, E, PACK * N], F32, name="raw")
         for e in range(E):
             nc.sync.dma_start(out=raw2[:, e, :], in_=w2[e].rearrange("(p j) n -> p (j n)", j=PACK))
-        grouped2 = keep.tile([P, E, PACK * N], BF16, name="last_pass2", align_bytes=64)
+        grouped2 = keep.tile([P, E - 1, PACK * N], BF16, name="last_pass2", align_bytes=64)
+        rounded2 = [grouped2[:, 0, :], grouped[:, 2 * H : 3 * H], grouped2[:, 1, :], grouped2[:, 2, :]]
         for e in range(E):
-            cast_down(grouped2[:, e, :], raw2[:, e, :])
-        down0 = quantise_kept(grouped2[:, 0, :], "down0", "down0")
-        last_h = ring.tile([P, PACK * H], BF16, name="grouped", align_bytes=64)
-        gate(up_banks, acts, [last_h[:, m * H : (m + 1) * H] for m in range(RANKS)])
-        down1 = quantise_kept(grouped2[:, 1, :], "down1", "last_pass0")
-        down23 = quantise_kept(grouped2[:, 2:, :].rearrange("p e x -> p (e x)"), "down23", "last_pass1")
-        hidden.append(quantise_kept(last_h[:, : RANKS * H], "hidden_last", "hidden_last"))
+            cast_down(nc.vector.tensor_copy if e == 1 else nc.scalar.copy, rounded2[e], raw2[:, e, :])
+        down = [quantise_kept(rounded2[e], "down%d" % e, "down%d" % e) for e in range(2)]
+        last = []
+        for m in range(RANKS):
+            gate(up_banks[m], acts[m], rounded2[2 * m])
+            down.append(quantise_kept(rounded2[2 + m], "down%d" % (2 + m), "down%d" % (2 + m)))
+            last.append(quantise_kept(rounded2[2 * m], "last%d" % m, "last%d" % m))
 
         by_rank = out.rearrange("n (m e u) -> n m e u", m=RANKS, e=E)
-        early = raw2[:, E - 1, :].rearrange("p (e m u) -> p e m u", m=RANKS, e=2)
-        for e, down in enumerate((down0, down1)):
-            y = second_layer(down, 0, hidden[e], 0, C)
-            nc.scalar.copy(out=early[:, e, :, :], in_=y.rearrange("p (m u) -> p m u", m=RANKS))
-            nc.sync.dma_start(out=by_rank[:, :, e, :], in_=early[:, e, :, :])
-        third = keep.tile([P, RANKS, HALF], F32, name="third")
-        y = second_layer(down23, 0, hidden[E - 2], 0, C)
-        nc.scalar.copy(out=third[:], in_=y.rearrange("p (m u) -> p m u", m=RANKS))
-        nc.sync.dma_start(out=by_rank[:, :, E - 2, :], in_=third[:])
+        for e in range(E - 1):
+            staged = keep.tile([P, RANKS, HALF], F32, name="staged%d" % e)[:]
+            y = psum_y.tile([P, C], F32, name="y")
+            second_layer(y[:], down[e], hidden[e])
+            nc.scalar.copy(out=staged, in_=y[:].rearrange("p (m u) -> p m u", m=RANKS))
+            nc.sync.dma_start(out=by_rank[:, :, e, :], in_=staged)
         for m in range(RANKS):
             late = keep.tile([P, HALF], F32, name="late%d" % m)
             copy = nc.scalar.copy if m == 0 else nc.vector.tensor_copy
-            copy(out=late[:], in_=second_layer(down23, N, hidden[E - 1], m * HALF, (m + 1) * HALF))
+            y = psum_y.tile([P, C], F32, name="y")
+            second_layer(y[:, :HALF], down[E - 1], last[m])
+            copy(out=late[:], in_=y[:, :HALF])
             nc.sync.dma_start(out=by_rank[:, m, E - 1, :], in_=late[:])

@@ -1,6 +1,7 @@
 from contextlib import ExitStack
 
 import concourse.mybir as mybir
+from concourse.masks import make_identity
 
 K, T, E, C, H, N = 1536, 1024, 4, 256, 512, 128
 RANKS = 2
@@ -27,7 +28,7 @@ WHOLE = 2
 GATE_SHARE = 32
 UP_SHARE = 64
 LAST_SHARE = 80
-LATE_SHARE = 40
+HALF_SHARES = (16, 32)
 
 
 def tile_moe_pke_glu_gelu_kernel(tc, x_words, x_scales, w1, w3, w2, offs, out):
@@ -37,12 +38,12 @@ def tile_moe_pke_glu_gelu_kernel(tc, x_words, x_scales, w1, w3, w2, offs, out):
         raws = ctx.enter_context(tc.tile_pool(name="raws", bufs=4))
         ring = ctx.enter_context(tc.tile_pool(name="ring", bufs=4))
         psum = ctx.enter_context(tc.psum_pool(name="psum", bufs=1))
-        psum_y = ctx.enter_context(tc.psum_pool(name="psum_y", bufs=4))
+        psum_y = ctx.enter_context(tc.psum_pool(name="psum_y", bufs=2))
 
         def weight_rows(index):
             return (w1, w3)[index % 2][index // 2].rearrange("(o p j) c -> p o (j c)", o=PASSES, j=PACK)
 
-        first_raw = raws.tile([P, PASSES, PACK * H], F32, name="raw")
+        first_raw = raws.tile([P, PASSES, PACK * H], F32, name="raw", align_bytes=64)
         nc.sync.dma_start(out=first_raw[:, 0, :], in_=weight_rows(0)[:, 0, :])
         offsets = keep.tile([P, E * C // 16], U16, name="offsets")
         nc.sync.dma_start(offsets[:], offs)
@@ -64,6 +65,9 @@ def tile_moe_pke_glu_gelu_kernel(tc, x_words, x_scales, w1, w3, w2, offs, out):
         nc.sync.dma_start(out=first_raw[:, 2, :], in_=weight_rows(0)[:, 2, :])
         token_words = [first_words[:]] + [later_words[:, o, :] for o in range(PASSES - 1)]
 
+        identity = keep.tile([P, P], F32, name="identity")
+        make_identity(nc, identity[:])
+
         slot_words = [keep.tile([P, E * C], U32, name="slot_words%d" % o, align_bytes=64) for o in range(PASSES)]
         slot_scales = keep.tile([P, E * C], U8, name="slot_scales", align_bytes=64)
 
@@ -77,11 +81,13 @@ def tile_moe_pke_glu_gelu_kernel(tc, x_words, x_scales, w1, w3, w2, offs, out):
                 passes = [keep.tile([P, PACK * H], F32, name="last_pass%d" % o, align_bytes=64)[:] for o in range(PASSES)]
                 for o in range(PASSES - 1):
                     nc.sync.dma_start(out=passes[o], in_=rows[:, o, :])
+                landing = passes[-1].rearrange("p (j c) -> p j c", j=PACK)
+                last = rows[:, PASSES - 1, :].rearrange("p (j c) -> p j c", j=PACK)
                 for half in range(2):
-                    cols = slice(half * 2 * H, (half + 1) * 2 * H)
-                    nc.sync.dma_start(out=passes[-1][:, cols], in_=rows[:, PASSES - 1, cols])
+                    cols = slice(half * H // 2, (half + 1) * H // 2)
+                    nc.sync.dma_start(out=landing[:, :, cols], in_=last[:, :, cols])
                 return passes
-            raw = raws.tile([P, PASSES, PACK * H], F32, name="raw")
+            raw = raws.tile([P, PASSES, PACK * H], F32, name="raw", align_bytes=64)
             if index < WHOLE:
                 cuts = [(0, PASSES)]
             elif index == WHOLE:
@@ -92,50 +98,52 @@ def tile_moe_pke_glu_gelu_kernel(tc, x_words, x_scales, w1, w3, w2, offs, out):
                 nc.sync.dma_start(out=raw[:, o0:o1, :], in_=rows[:, o0:o1, :])
             return [raw[:, o, :] for o in range(PASSES)]
 
-        def cast(src, dst, m0, cut, m1):
-            nc.scalar.copy(out=dst[:, cut:m1, :, :], in_=src[:, cut:m1, :, :])
-            nc.vector.tensor_copy(out=dst[:, m0:cut, :, :], in_=src[:, m0:cut, :, :])
-
         def quantise(raw_pass, grouped, codes, scales, share, in_halves):
-            src = raw_pass.rearrange("p (j m t) -> p m j t", j=PACK, t=PACK)
-            dst = grouped.rearrange("p (t m j) -> p m j t", t=PACK, j=PACK)
+            src = raw_pass.rearrange("p (j c i) -> p c j i", j=PACK, i=4)
+            dst = grouped.rearrange("p (c i j) -> p c j i", i=4, j=PACK)
             if not in_halves:
-                cast(src, dst, 0, share, P)
+                nc.scalar.copy(out=dst[:, share:, :, :], in_=src[:, share:, :, :])
+                nc.vector.tensor_copy(out=dst[:, :share, :, :], in_=src[:, :share, :, :])
                 nc.vector.quantize_mx(out=codes.bitcast(FP8X4), scales=scales, in_=grouped)
                 return
-            cast(src[:, :, :2, :], dst[:, :, :2, :], 0, share, P)
-            nc.scalar.copy(out=dst[:, LATE_SHARE:, 2:, 2:], in_=src[:, LATE_SHARE:, 2:, 2:])
-            nc.vector.tensor_copy(out=dst[:, :, 2:, :2], in_=src[:, :, 2:, :2])
-            nc.vector.tensor_copy(out=dst[:, :LATE_SHARE, 2:, 2:], in_=src[:, :LATE_SHARE, 2:, 2:])
-            for t in range(PACK):
-                c0, c1 = t * P, (t + 1) * P
+            for half in range(2):
+                g0, g1 = half * P // 2, (half + 1) * P // 2
+                cut = g0 + HALF_SHARES[half]
+                nc.scalar.copy(out=dst[:, cut:g1, :, :], in_=src[:, cut:g1, :, :])
+                nc.vector.tensor_copy(out=dst[:, g0:cut, :, :], in_=src[:, g0:cut, :, :])
+                c0, c1 = half * H // 2, (half + 1) * H // 2
                 nc.vector.quantize_mx(
                     out=codes[:, c0:c1].bitcast(FP8X4), scales=scales[:, c0:c1], in_=grouped[:, PACK * c0 : PACK * c1]
                 )
 
-        def multiply(banks, e, o, codes, scales):
-            for m in range(RANKS):
-                cols = slice(e * C + m * HALF, e * C + (m + 1) * HALF)
-                for t in range(PACK):
-                    nc.tensor.matmul_mx(
-                        out=banks[m][:, t, :],
-                        lhsT=codes[:, t * P : (t + 1) * P].bitcast(FP8X4),
-                        lhsT_scale=scales[:, t * P : (t + 1) * P],
-                        rhs=slot_words[o][:, cols].bitcast(FP8X4),
-                        rhs_scale=slot_scales[4 * o : P, cols],
-                        start=(o == 0 and t == 0),
-                        stop=(o == PASSES - 1 and t == PACK - 1),
-                    )
-
-        def activate(bank, spent):
-            act = spent[:, :H].rearrange("p (u t) -> p u t", t=PACK)
-            nc.scalar.activation(out=act, in_=bank[:].rearrange("p t u -> p u t"), func=GELU)
-            return act
-
-        def gate(bank, act, values):
-            nc.vector.tensor_tensor(
-                out=values.rearrange("p (u t) -> p u t", t=PACK), in0=bank[:].rearrange("p t u -> p u t"), in1=act, op=MULT
+        def product(sums, e, m, o, codes, scales, start, stop):
+            cols = slice(e * C + m * HALF, e * C + (m + 1) * HALF)
+            nc.tensor.matmul_mx(
+                out=sums,
+                lhsT=slot_words[o][:, cols].bitcast(FP8X4),
+                lhsT_scale=slot_scales[4 * o : P, cols],
+                rhs=codes.bitcast(FP8X4),
+                rhs_scale=scales,
+                start=start,
+                stop=stop,
             )
+
+        def multiply(banks, e, o, codes, scales, by_halves):
+            if not by_halves:
+                for m in range(RANKS):
+                    product(banks[m][:], e, m, o, codes, scales, o == 0, o == PASSES - 1)
+                return
+            for half in range(2):
+                cols = slice(half * H // 2, (half + 1) * H // 2)
+                for m in range(RANKS):
+                    sums = banks[half][:, m * H // 2 : (m + 1) * H // 2]
+                    start, stop = o == 0 and m == 0, o == PASSES - 1 and m == RANKS - 1
+                    product(sums, e, m, o, codes[:, cols], scales[:, cols], start, stop)
+
+        def turn(turned, values):
+            pairs = values.bitcast(F32)
+            for u in range(2):
+                nc.tensor.transpose(turned[:, u, :], pairs[:, u : H // 2 : 2], identity[:])
 
         def quantise_kept(values, name, codes_tag):
             width = values.shape[1] // PACK
@@ -153,8 +161,8 @@ def tile_moe_pke_glu_gelu_kernel(tc, x_words, x_scales, w1, w3, w2, offs, out):
         def second_layer(y, weights, slots):
             nc.tensor.matmul_mx(
                 out=y,
-                lhsT=weights[0][:].bitcast(FP8X4),
-                lhsT_scale=weights[1][:],
+                lhsT=weights[0].bitcast(FP8X4),
+                lhsT_scale=weights[1],
                 rhs=slots[0][:].bitcast(FP8X4),
                 rhs_scale=slots[1][:],
                 start=True,
@@ -165,52 +173,80 @@ def tile_moe_pke_glu_gelu_kernel(tc, x_words, x_scales, w1, w3, w2, offs, out):
         acts = {}
         for index in range(MATRICES):
             e, is_up = divmod(index, 2)
+            is_last = index == MATRICES - 1
             passes = load(index) if index else [first_raw[:, o, :] for o in range(PASSES)]
-            banks = [psum.tile([P, PACK, HALF], F32, name="%s%d" % (("gate", "up")[is_up], m)) for m in range(RANKS)]
+            banks = [psum.tile([P, H], F32, name="%s%d" % (("gate", "up")[is_up], m)) for m in range(RANKS)]
             for o in range(PASSES):
                 grouped = ring.tile([P, PACK * H], BF16, name="grouped", align_bytes=64)
                 codes = ring.tile([P, H], U32, name="codes", align_bytes=64)
                 scales = ring.tile([P, H], U8, name="scales", align_bytes=64)
-                is_last = index == MATRICES - 1
                 if index * PASSES + o >= CHUNKS - 4:
                     share = LAST_SHARE
                 else:
-                    share = UP_SHARE if is_up or o == PASSES - 1 else GATE_SHARE
+                    share = UP_SHARE if is_up or o > 0 else GATE_SHARE
                 quantise(passes[o], grouped[:], codes[:], scales[:], share, is_last and o == PASSES - 1)
                 if index == 0 or (is_up and not is_last):
                     gather(slot_words[o], token_words[o].bitcast(U32), e + is_up)
                     if o == 0:
                         gather(slot_scales, token_scales[:], e + is_up)
-                multiply(banks, e, o, codes[:], scales[:])
-                if is_up and o < RANKS:
-                    acts[o] = activate(gate_banks[o], passes[o])
+                multiply(banks, e, o, codes[:], scales[:], is_last)
+                for m in range(RANKS):
+                    if is_up and o == (0 if is_last else m):
+                        acts[m] = passes[o][:, m * H : (m + 1) * H]
+                        nc.scalar.activation(out=acts[m], in_=gate_banks[m][:], func=GELU)
                 if o == 0 and not is_up and e > 0:
+                    turned = psum_y.tile([P, RANKS, 2, HALF], F32, name="turned")
                     for m in range(RANKS):
-                        gate(up_banks[m], acts[m], grouped[:, m * H : (m + 1) * H])
-                    hidden.append(quantise_kept(grouped[:, : RANKS * H], "hidden%d" % e, "hidden%d" % e))
+                        values = grouped[:, m * H : (m + 1) * H]
+                        nc.vector.tensor_tensor(out=values, in0=up_banks[m][:], in1=acts[m], op=MULT)
+                        turn(turned[:, m, :, :], values)
+                if o == PASSES - 1 and not is_up and e > 0:
+                    woven = passes[o][:, :H]
+                    nc.scalar.copy(
+                        out=woven.rearrange("p (m s u) -> p m s u", m=RANKS, u=2), in_=turned[:].rearrange("p m u s -> p m s u")
+                    )
+                    hidden.append(quantise_kept(woven.bitcast(BF16), "hidden%d" % e, "hidden%d" % e))
             if is_up:
                 up_banks = banks
             else:
                 gate_banks = banks
 
-        raw2 = raws.tile([P, E, PACK * N], F32, name="raw")
+        raw2 = raws.tile([P, E, PACK * N], F32, name="raw", align_bytes=64)
         for e in range(E):
             nc.sync.dma_start(out=raw2[:, e, :], in_=w2[e].rearrange("(p j) n -> p (j n)", j=PACK))
-        grouped2 = keep.tile([P, E - 1, PACK * N], BF16, name="last_pass2", align_bytes=64)
-        rounded2 = [grouped2[:, 0, :], grouped[:, 2 * H : 3 * H], grouped2[:, 1, :], grouped2[:, 2, :]]
+        rounded2 = keep.tile([P, E, PACK * N], BF16, name="last_pass2", align_bytes=64)
         for e in range(E):
-            cast_down(nc.vector.tensor_copy if e == 1 else nc.scalar.copy, rounded2[e], raw2[:, e, :])
-        down = [quantise_kept(rounded2[e], "down%d" % e, "down%d" % e) for e in range(2)]
-        last = []
+            cast_down(nc.vector.tensor_copy if e == 1 else nc.scalar.copy, rounded2[:, e, :], raw2[:, e, :])
+
+        values = grouped[:, RANKS * H :].rearrange("p (m c) -> p m c", m=RANKS)
+        turned = [psum_y.tile([P, 2, HALF], F32, name="turned") for m in range(RANKS)]
+        for half in range(2):
+            cols = slice(half * H // 2, (half + 1) * H // 2)
+            for m in range(RANKS):
+                sums = up_banks[half][:, m * H // 2 : (m + 1) * H // 2]
+                nc.vector.tensor_tensor(out=values[:, m, cols], in0=sums, in1=acts[m][:, cols], op=MULT)
         for m in range(RANKS):
-            gate(up_banks[m], acts[m], rounded2[2 * m])
-            down.append(quantise_kept(rounded2[2 + m], "down%d" % (2 + m), "down%d" % (2 + m)))
-            last.append(quantise_kept(rounded2[2 * m], "last%d" % m, "last%d" % m))
+            turn(turned[m][:], values[:, m, :])
+        down_codes = keep.tile([P, E * N], U32, name="last_pass0", align_bytes=64)
+        down_scales = keep.tile([P, E * N], U8, name="down_scales", align_bytes=64)
+        for g in range(2):
+            cols = slice(2 * g * N, 2 * (g + 1) * N)
+            nc.vector.quantize_mx(
+                out=down_codes[:, cols].bitcast(FP8X4),
+                scales=down_scales[:, cols],
+                in_=rounded2[:, 2 * g : 2 * g + 2, :].rearrange("p e x -> p (e x)"),
+            )
+        down = [[plane[:, e * N : (e + 1) * N] for plane in (down_codes, down_scales)] for e in range(E)]
+        woven = [keep.tile([P, HALF * 2], F32, name="woven%d" % m, align_bytes=64) for m in range(RANKS)]
+        for m in range(RANKS):
+            copy = nc.scalar.copy if m == 0 else nc.vector.tensor_copy
+            copy(out=woven[m][:].rearrange("p (s u) -> p s u", u=2), in_=turned[m][:].rearrange("p u s -> p s u"))
+        last = [quantise_kept(woven[m][:].bitcast(BF16), "last%d" % m, "last%d" % m) for m in range(RANKS)]
 
         by_rank = out.rearrange("n (m e u) -> n m e u", m=RANKS, e=E)
         for e in range(E - 1):
             staged = keep.tile([P, RANKS, HALF], F32, name="staged%d" % e)[:]
-            y = psum_y.tile([P, C], F32, name="y")
+            y = psum.tile([P, C], F32, name=("gate0", "gate1", "up0")[e])
             second_layer(y[:], down[e], hidden[e])
             nc.scalar.copy(out=staged, in_=y[:].rearrange("p (m u) -> p m u", m=RANKS))
             nc.sync.dma_start(out=by_rank[:, :, e, :], in_=staged)

@@ -23,12 +23,11 @@ K_PASS = P * PACK
 PASSES = K // K_PASS
 HALF = C // RANKS
 MATRICES = 2 * E
-CHUNKS = MATRICES * PASSES
 WHOLE = 2
-GATE_SHARE = 32
-UP_SHARE = 64
-LAST_SHARE = 80
-HALF_SHARES = (16, 32)
+GATE_SHARES = (0, 48, 64)
+UP_SHARE = 72
+LAST_SHARE = 88
+HALF_SHARES = (16, 28)
 
 
 def tile_moe_pke_glu_gelu_kernel(tc, x_words, x_scales, w1, w3, w2, offs, out):
@@ -103,7 +102,8 @@ def tile_moe_pke_glu_gelu_kernel(tc, x_words, x_scales, w1, w3, w2, offs, out):
             dst = grouped.rearrange("p (c i j) -> p c j i", i=4, j=PACK)
             if not in_halves:
                 nc.scalar.copy(out=dst[:, share:, :, :], in_=src[:, share:, :, :])
-                nc.vector.tensor_copy(out=dst[:, :share, :, :], in_=src[:, :share, :, :])
+                if share:
+                    nc.vector.tensor_copy(out=dst[:, :share, :, :], in_=src[:, :share, :, :])
                 nc.vector.quantize_mx(out=codes.bitcast(FP8X4), scales=scales, in_=grouped)
                 return
             for half in range(2):
@@ -180,10 +180,15 @@ def tile_moe_pke_glu_gelu_kernel(tc, x_words, x_scales, w1, w3, w2, offs, out):
                 grouped = ring.tile([P, PACK * H], BF16, name="grouped", align_bytes=64)
                 codes = ring.tile([P, H], U32, name="codes", align_bytes=64)
                 scales = ring.tile([P, H], U8, name="scales", align_bytes=64)
-                if index * PASSES + o >= CHUNKS - 4:
+                if is_last and o == 1:
                     share = LAST_SHARE
                 else:
-                    share = UP_SHARE if is_up or o > 0 else GATE_SHARE
+                    share = UP_SHARE if is_up else GATE_SHARES[o]
+                if o == 0 and not is_up and e > 0:
+                    turned = psum_y.tile([P, RANKS, 2, HALF], F32, name="turned")
+                    values = ring.tile([P, RANKS, H], BF16, name="values", bufs=1)
+                    for m in range(RANKS):
+                        nc.vector.tensor_tensor(out=values[:, m, :], in0=up_banks[m][:], in1=acts[m], op=MULT)
                 quantise(passes[o], grouped[:], codes[:], scales[:], share, is_last and o == PASSES - 1)
                 if index == 0 or (is_up and not is_last):
                     gather(slot_words[o], token_words[o].bitcast(U32), e + is_up)
@@ -195,12 +200,9 @@ def tile_moe_pke_glu_gelu_kernel(tc, x_words, x_scales, w1, w3, w2, offs, out):
                         acts[m] = passes[o][:, m * H : (m + 1) * H]
                         nc.scalar.activation(out=acts[m], in_=gate_banks[m][:], func=GELU)
                 if o == 0 and not is_up and e > 0:
-                    turned = psum_y.tile([P, RANKS, 2, HALF], F32, name="turned")
                     for m in range(RANKS):
-                        values = grouped[:, m * H : (m + 1) * H]
-                        nc.vector.tensor_tensor(out=values, in0=up_banks[m][:], in1=acts[m], op=MULT)
-                        turn(turned[:, m, :, :], values)
-                if o == PASSES - 1 and not is_up and e > 0:
+                        turn(turned[:, m, :, :], values[:, m, :])
+                if o == 1 and not is_up and e > 0:
                     woven = passes[o][:, :H]
                     nc.scalar.copy(
                         out=woven.rearrange("p (m s u) -> p m s u", m=RANKS, u=2), in_=turned[:].rearrange("p m u s -> p m s u")
@@ -216,27 +218,21 @@ def tile_moe_pke_glu_gelu_kernel(tc, x_words, x_scales, w1, w3, w2, offs, out):
             nc.sync.dma_start(out=raw2[:, e, :], in_=w2[e].rearrange("(p j) n -> p (j n)", j=PACK))
         rounded2 = keep.tile([P, E, PACK * N], BF16, name="last_pass2", align_bytes=64)
         for e in range(E):
-            cast_down(nc.vector.tensor_copy if e == 1 else nc.scalar.copy, rounded2[:, e, :], raw2[:, e, :])
+            cast_down(nc.scalar.copy, rounded2[:, e, :], raw2[:, e, :])
 
         values = grouped[:, RANKS * H :].rearrange("p (m c) -> p m c", m=RANKS)
         turned = [psum_y.tile([P, 2, HALF], F32, name="turned") for m in range(RANKS)]
+        down = []
         for half in range(2):
             cols = slice(half * H // 2, (half + 1) * H // 2)
             for m in range(RANKS):
                 sums = up_banks[half][:, m * H // 2 : (m + 1) * H // 2]
                 nc.vector.tensor_tensor(out=values[:, m, cols], in0=sums, in1=acts[m][:, cols], op=MULT)
+            pair = rounded2[:, 2 * half : 2 * half + 2, :].rearrange("p e x -> p (e x)")
+            planes = quantise_kept(pair, "down%d" % half, ("down0", "last_pass0")[half])
+            down.extend([plane[:, i * N : (i + 1) * N] for plane in planes] for i in range(2))
         for m in range(RANKS):
             turn(turned[m][:], values[:, m, :])
-        down_codes = keep.tile([P, E * N], U32, name="last_pass0", align_bytes=64)
-        down_scales = keep.tile([P, E * N], U8, name="down_scales", align_bytes=64)
-        for g in range(2):
-            cols = slice(2 * g * N, 2 * (g + 1) * N)
-            nc.vector.quantize_mx(
-                out=down_codes[:, cols].bitcast(FP8X4),
-                scales=down_scales[:, cols],
-                in_=rounded2[:, 2 * g : 2 * g + 2, :].rearrange("p e x -> p (e x)"),
-            )
-        down = [[plane[:, e * N : (e + 1) * N] for plane in (down_codes, down_scales)] for e in range(E)]
         woven = [keep.tile([P, HALF * 2], F32, name="woven%d" % m, align_bytes=64) for m in range(RANKS)]
         for m in range(RANKS):
             copy = nc.scalar.copy if m == 0 else nc.vector.tensor_copy

@@ -27,7 +27,8 @@ WHOLE = 2
 GATE_SHARES = (0, 48, 64)
 UP_SHARE = 72
 LAST_SHARE = 88
-HALF_SHARES = (16, 28)
+PIECE_SHARE = 40
+LAST_PIECES = ((0, H // 2), (H // 2, H - N), (H - N, H))
 
 
 def tile_moe_pke_glu_gelu_kernel(tc, x_words, x_scales, w1, w3, w2, offs, out):
@@ -82,8 +83,7 @@ def tile_moe_pke_glu_gelu_kernel(tc, x_words, x_scales, w1, w3, w2, offs, out):
                     nc.sync.dma_start(out=passes[o], in_=rows[:, o, :])
                 landing = passes[-1].rearrange("p (j c) -> p j c", j=PACK)
                 last = rows[:, PASSES - 1, :].rearrange("p (j c) -> p j c", j=PACK)
-                for half in range(2):
-                    cols = slice(half * H // 2, (half + 1) * H // 2)
+                for cols in (slice(0, H - N), slice(H - N, H)):
                     nc.sync.dma_start(out=landing[:, :, cols], in_=last[:, :, cols])
                 return passes
             raw = raws.tile([P, PASSES, PACK * H], F32, name="raw", align_bytes=64)
@@ -106,12 +106,12 @@ def tile_moe_pke_glu_gelu_kernel(tc, x_words, x_scales, w1, w3, w2, offs, out):
                     nc.vector.tensor_copy(out=dst[:, :share, :, :], in_=src[:, :share, :, :])
                 nc.vector.quantize_mx(out=codes.bitcast(FP8X4), scales=scales, in_=grouped)
                 return
-            for half in range(2):
-                g0, g1 = half * P // 2, (half + 1) * P // 2
-                cut = g0 + HALF_SHARES[half]
-                nc.scalar.copy(out=dst[:, cut:g1, :, :], in_=src[:, cut:g1, :, :])
-                nc.vector.tensor_copy(out=dst[:, g0:cut, :, :], in_=src[:, g0:cut, :, :])
-                c0, c1 = half * H // 2, (half + 1) * H // 2
+            nc.scalar.copy(out=dst[:, share:64, :, :], in_=src[:, share:64, :, :])
+            nc.vector.tensor_copy(out=dst[:, :share, :, :], in_=src[:, :share, :, :])
+            nc.scalar.copy(out=dst[:, 64:96, :, :], in_=src[:, 64:96, :, :])
+            for c0, c1 in LAST_PIECES:
+                if c1 == H:
+                    nc.vector.tensor_copy(out=dst[:, 96:, :, :], in_=src[:, 96:, :, :])
                 nc.vector.quantize_mx(
                     out=codes[:, c0:c1].bitcast(FP8X4), scales=scales[:, c0:c1], in_=grouped[:, PACK * c0 : PACK * c1]
                 )
@@ -133,12 +133,12 @@ def tile_moe_pke_glu_gelu_kernel(tc, x_words, x_scales, w1, w3, w2, offs, out):
                 for m in range(RANKS):
                     product(banks[m][:], e, m, o, codes, scales, o == 0, o == PASSES - 1)
                 return
-            for half in range(2):
-                cols = slice(half * H // 2, (half + 1) * H // 2)
+            for c0, c1 in LAST_PIECES if o == PASSES - 1 else ((0, H // 2), (H // 2, H)):
+                half, first = divmod(c0, H // 2)
                 for m in range(RANKS):
-                    sums = banks[half][:, m * H // 2 : (m + 1) * H // 2]
-                    start, stop = o == 0 and m == 0, o == PASSES - 1 and m == RANKS - 1
-                    product(sums, e, m, o, codes[:, cols], scales[:, cols], start, stop)
+                    sums = banks[half][:, m * H // 2 + first : m * H // 2 + first + c1 - c0]
+                    start, stop = o == 0 and m == 0, o == PASSES - 1 and m == RANKS - 1 and c1 % (H // 2) == 0
+                    product(sums, e, m, o, codes[:, c0:c1], scales[:, c0:c1], start, stop)
 
         def turn(turned, values):
             pairs = values.bitcast(F32)
@@ -180,8 +180,8 @@ def tile_moe_pke_glu_gelu_kernel(tc, x_words, x_scales, w1, w3, w2, offs, out):
                 grouped = ring.tile([P, PACK * H], BF16, name="grouped", align_bytes=64)
                 codes = ring.tile([P, H], U32, name="codes", align_bytes=64)
                 scales = ring.tile([P, H], U8, name="scales", align_bytes=64)
-                if is_last and o == 1:
-                    share = LAST_SHARE
+                if is_last and o > 0:
+                    share = LAST_SHARE if o == 1 else PIECE_SHARE
                 else:
                     share = UP_SHARE if is_up else GATE_SHARES[o]
                 if o == 0 and not is_up and e > 0:
@@ -239,17 +239,20 @@ def tile_moe_pke_glu_gelu_kernel(tc, x_words, x_scales, w1, w3, w2, offs, out):
             copy(out=woven[m][:].rearrange("p (s u) -> p s u", u=2), in_=turned[m][:].rearrange("p u s -> p s u"))
         last = [quantise_kept(woven[m][:].bitcast(BF16), "last%d" % m, "last%d" % m) for m in range(RANKS)]
 
-        by_rank = out.rearrange("n (m e u) -> n m e u", m=RANKS, e=E)
-        for e in range(E - 1):
-            staged = keep.tile([P, RANKS, HALF], F32, name="staged%d" % e)[:]
-            y = psum.tile([P, C], F32, name=("gate0", "gate1", "up0")[e])
-            second_layer(y[:], down[e], hidden[e])
-            nc.scalar.copy(out=staged, in_=y[:].rearrange("p (m u) -> p m u", m=RANKS))
-            nc.sync.dma_start(out=by_rank[:, :, e, :], in_=staged)
+        by_rank = out.rearrange("n (m x) -> n m x", m=RANKS)
+        early = keep.tile([P, RANKS, 2, HALF], F32, name="early")
+        y = psum.tile([P, 2, C], F32, name="gate0")
+        for e in range(2):
+            second_layer(y[:, e, :], down[e], hidden[e])
+        nc.scalar.copy(out=early[:], in_=y[:].rearrange("p e (m u) -> p m e u", m=RANKS))
+        nc.sync.dma_start(out=by_rank[:, :, :C], in_=early[:].rearrange("p m e u -> p m (e u)"))
+        late = keep.tile([P, RANKS, 2, HALF], F32, name="late")
+        y = psum.tile([P, C], F32, name="gate1")
+        second_layer(y[:], down[E - 2], hidden[E - 2])
+        nc.scalar.copy(out=late[:, :, 0, :], in_=y[:].rearrange("p (m u) -> p m u", m=RANKS))
         for m in range(RANKS):
-            late = keep.tile([P, HALF], F32, name="late%d" % m)
             copy = nc.scalar.copy if m == 0 else nc.vector.tensor_copy
-            y = psum_y.tile([P, C], F32, name="y")
-            second_layer(y[:, :HALF], down[E - 1], last[m])
-            copy(out=late[:], in_=y[:, :HALF])
-            nc.sync.dma_start(out=by_rank[:, m, E - 1, :], in_=late[:])
+            y = psum_y.tile([P, HALF], F32, name="y")
+            second_layer(y[:], down[E - 1], last[m])
+            copy(out=late[:, m, 1, :], in_=y[:])
+            nc.sync.dma_start(out=by_rank[:, m, C:], in_=late[:, m, :, :].rearrange("p e u -> p (e u)"))

@@ -214,25 +214,36 @@ def tile_moe_pke_glu_gelu_kernel(tc, x_words, x_scales, w1, w3, w2, offs, out):
                 gate_banks = banks
 
         raw2 = raws.tile([P, E, PACK * N], F32, name="raw", align_bytes=64)
-        for e in range(E):
-            nc.sync.dma_start(out=raw2[:, e, :], in_=w2[e].rearrange("(p j) n -> p (j n)", j=PACK))
-        rounded2 = keep.tile([P, E, PACK * N], BF16, name="last_pass2", align_bytes=64)
-        for e in range(E):
-            cast_down(nc.scalar.copy, rounded2[:, e, :], raw2[:, e, :])
+        order = (0, 1, 3, 2)
+        for place, e in enumerate(order):
+            nc.sync.dma_start(out=raw2[:, place, :], in_=w2[e].rearrange("(p j) n -> p (j n)", j=PACK))
+        rounded2 = keep.tile([P, E - 1, PACK * N], BF16, name="last_pass2", align_bytes=64)
+        for place in range(E - 1):
+            cast_down(nc.scalar.copy, rounded2[:, place, :], raw2[:, place, :])
 
         values = grouped[:, RANKS * H :].rearrange("p (m c) -> p m c", m=RANKS)
         turned = [psum_y.tile([P, 2, HALF], F32, name="turned") for m in range(RANKS)]
-        down = []
         for half in range(2):
             cols = slice(half * H // 2, (half + 1) * H // 2)
             for m in range(RANKS):
                 sums = up_banks[half][:, m * H // 2 : (m + 1) * H // 2]
                 nc.vector.tensor_tensor(out=values[:, m, cols], in0=sums, in1=acts[m][:, cols], op=MULT)
-            pair = rounded2[:, 2 * half : 2 * half + 2, :].rearrange("p e x -> p (e x)")
-            planes = quantise_kept(pair, "down%d" % half, ("down0", "last_pass0")[half])
-            down.extend([plane[:, i * N : (i + 1) * N] for plane in planes] for i in range(2))
         for m in range(RANKS):
             turn(turned[m][:], values[:, m, :])
+        down_codes = keep.tile([P, E * N], U32, name="last_pass0", align_bytes=64)
+        down_scales = keep.tile([P, E * N], U8, name="down_scales", align_bytes=64)
+
+        def quantise_down(place, rounded):
+            cols = slice(place * N, place * N + rounded.shape[1] // PACK)
+            nc.vector.quantize_mx(out=down_codes[:, cols].bitcast(FP8X4), scales=down_scales[:, cols], in_=rounded)
+
+        quantise_down(0, rounded2[:, :2, :].rearrange("p e x -> p (e x)"))
+        quantise_down(2, rounded2[:, 2, :])
+        cast_down(nc.vector.tensor_copy, values[:, 0, :], raw2[:, E - 1, :])
+        quantise_down(E - 1, values[:, 0, :])
+        down = {
+            e: [plane[:, place * N : (place + 1) * N] for plane in (down_codes, down_scales)] for place, e in enumerate(order)
+        }
         woven = [keep.tile([P, HALF * 2], F32, name="woven%d" % m, align_bytes=64) for m in range(RANKS)]
         for m in range(RANKS):
             copy = nc.scalar.copy if m == 0 else nc.vector.tensor_copy

@@ -78,14 +78,16 @@ def tile_moe_pke_glu_gelu_kernel(tc, x_words, x_scales, w1, w3, w2, offs, out):
         def load(index):
             rows = weight_rows(index)
             if index == MATRICES - 1:
-                passes = [keep.tile([P, PACK * H], F32, name="last_pass%d" % o, align_bytes=64)[:] for o in range(PASSES)]
+                passes = [keep.tile([P, PACK * H], F32, name="last_pass%d" % o, align_bytes=64)[:] for o in range(PASSES - 1)]
                 for o in range(PASSES - 1):
                     nc.sync.dma_start(out=passes[o], in_=rows[:, o, :])
-                landing = passes[-1].rearrange("p (j c) -> p j c", j=PACK)
                 last = rows[:, PASSES - 1, :].rearrange("p (j c) -> p j c", j=PACK)
-                for cols in (slice(0, H - N), slice(H - N, H)):
-                    nc.sync.dma_start(out=landing[:, :, cols], in_=last[:, :, cols])
-                return passes
+                landed = []
+                for name, c0, c1 in (("last_pass2", 0, H - N), ("last_piece", H - N, H)):
+                    piece = keep.tile([P, PACK, c1 - c0], F32, name=name, align_bytes=64)
+                    nc.sync.dma_start(out=piece[:], in_=last[:, :, c0:c1])
+                    landed.append(piece[:].rearrange("p j (c i) -> p c j i", i=4))
+                return passes + [landed]
             raw = raws.tile([P, PASSES, PACK * H], F32, name="raw", align_bytes=64)
             if index < WHOLE:
                 cuts = [(0, PASSES)]
@@ -98,23 +100,29 @@ def tile_moe_pke_glu_gelu_kernel(tc, x_words, x_scales, w1, w3, w2, offs, out):
             return [raw[:, o, :] for o in range(PASSES)]
 
         def quantise(raw_pass, grouped, codes, scales, share, in_halves):
-            src = raw_pass.rearrange("p (j c i) -> p c j i", j=PACK, i=4)
             dst = grouped.rearrange("p (c i j) -> p c j i", i=4, j=PACK)
             if not in_halves:
+                src = raw_pass.rearrange("p (j c i) -> p c j i", j=PACK, i=4)
                 nc.scalar.copy(out=dst[:, share:, :, :], in_=src[:, share:, :, :])
                 if share:
                     nc.vector.tensor_copy(out=dst[:, :share, :, :], in_=src[:, :share, :, :])
                 nc.vector.quantize_mx(out=codes.bitcast(FP8X4), scales=scales, in_=grouped)
-                return
+                return [codes[:, c0:c1] for c0, c1 in LAST_PIECES]
+            src, final = raw_pass
             nc.scalar.copy(out=dst[:, share:64, :, :], in_=src[:, share:64, :, :])
             nc.vector.tensor_copy(out=dst[:, :share, :, :], in_=src[:, :share, :, :])
             nc.scalar.copy(out=dst[:, 64:96, :, :], in_=src[:, 64:96, :, :])
+            piece_codes = []
             for c0, c1 in LAST_PIECES:
-                if c1 == H:
-                    nc.vector.tensor_copy(out=dst[:, 96:, :, :], in_=src[:, 96:, :, :])
+                if c1 == H - N:
+                    nc.vector.tensor_copy(out=dst[:, 96:, :, :], in_=final)
+                    piece_codes.append(keep.tile([P, N], U32, name="last_piece", align_bytes=64)[:])
+                else:
+                    piece_codes.append(codes[:, c0:c1])
                 nc.vector.quantize_mx(
-                    out=codes[:, c0:c1].bitcast(FP8X4), scales=scales[:, c0:c1], in_=grouped[:, PACK * c0 : PACK * c1]
+                    out=piece_codes[-1].bitcast(FP8X4), scales=scales[:, c0:c1], in_=grouped[:, PACK * c0 : PACK * c1]
                 )
+            return piece_codes
 
         def product(sums, e, m, o, codes, scales, start, stop):
             cols = slice(e * C + m * HALF, e * C + (m + 1) * HALF)
@@ -128,17 +136,15 @@ def tile_moe_pke_glu_gelu_kernel(tc, x_words, x_scales, w1, w3, w2, offs, out):
                 stop=stop,
             )
 
-        def multiply(banks, e, o, codes, scales, by_halves):
+        def multiply(banks, e, o, codes, scales, by_halves, piece_codes):
             if not by_halves:
                 for m in range(RANKS):
                     product(banks[m][:], e, m, o, codes, scales, o == 0, o == PASSES - 1)
                 return
-            for c0, c1 in LAST_PIECES if o == PASSES - 1 else ((0, H // 2), (H // 2, H)):
-                half, first = divmod(c0, H // 2)
+            for bank, piece, (c0, c1) in zip(banks, piece_codes, LAST_PIECES):
                 for m in range(RANKS):
-                    sums = banks[half][:, m * H // 2 + first : m * H // 2 + first + c1 - c0]
-                    start, stop = o == 0 and m == 0, o == PASSES - 1 and m == RANKS - 1 and c1 % (H // 2) == 0
-                    product(sums, e, m, o, codes[:, c0:c1], scales[:, c0:c1], start, stop)
+                    start, stop = o == 0 and m == 0, o == PASSES - 1 and m == RANKS - 1
+                    product(bank[:, m, :], e, m, o, piece, scales[:, c0:c1], start, stop)
 
         def turn(turned, values):
             pairs = values.bitcast(F32)
@@ -163,8 +169,8 @@ def tile_moe_pke_glu_gelu_kernel(tc, x_words, x_scales, w1, w3, w2, offs, out):
                 out=y,
                 lhsT=weights[0].bitcast(FP8X4),
                 lhsT_scale=weights[1],
-                rhs=slots[0][:].bitcast(FP8X4),
-                rhs_scale=slots[1][:],
+                rhs=slots[0].bitcast(FP8X4),
+                rhs_scale=slots[1],
                 start=True,
                 stop=True,
             )
@@ -175,7 +181,11 @@ def tile_moe_pke_glu_gelu_kernel(tc, x_words, x_scales, w1, w3, w2, offs, out):
             e, is_up = divmod(index, 2)
             is_last = index == MATRICES - 1
             passes = load(index) if index else [first_raw[:, o, :] for o in range(PASSES)]
-            banks = [psum.tile([P, H], F32, name="%s%d" % (("gate", "up")[is_up], m)) for m in range(RANKS)]
+            if is_last:
+                banks = [psum.tile([P, RANKS, c1 - c0], F32, name="up%d" % m) for m, (c0, c1) in enumerate(LAST_PIECES[:2])]
+                banks.append(psum_y.tile([P, RANKS, N], F32, name="y"))
+            else:
+                banks = [psum.tile([P, H], F32, name="%s%d" % (("gate", "up")[is_up], m)) for m in range(RANKS)]
             for o in range(PASSES):
                 grouped = ring.tile([P, PACK * H], BF16, name="grouped", align_bytes=64)
                 codes = ring.tile([P, H], U32, name="codes", align_bytes=64)
@@ -189,12 +199,12 @@ def tile_moe_pke_glu_gelu_kernel(tc, x_words, x_scales, w1, w3, w2, offs, out):
                     values = ring.tile([P, RANKS, H], BF16, name="values", bufs=1)
                     for m in range(RANKS):
                         nc.vector.tensor_tensor(out=values[:, m, :], in0=up_banks[m][:], in1=acts[m], op=MULT)
-                quantise(passes[o], grouped[:], codes[:], scales[:], share, is_last and o == PASSES - 1)
+                piece_codes = quantise(passes[o], grouped[:], codes[:], scales[:], share, is_last and o == PASSES - 1)
                 if index == 0 or (is_up and not is_last):
                     gather(slot_words[o], token_words[o].bitcast(U32), e + is_up)
                     if o == 0:
                         gather(slot_scales, token_scales[:], e + is_up)
-                multiply(banks, e, o, codes[:], scales[:], is_last)
+                multiply(banks, e, o, codes[:], scales[:], is_last, piece_codes)
                 for m in range(RANKS):
                     if is_up and o == (0 if is_last else m):
                         acts[m] = passes[o][:, m * H : (m + 1) * H]
@@ -207,63 +217,69 @@ def tile_moe_pke_glu_gelu_kernel(tc, x_words, x_scales, w1, w3, w2, offs, out):
                     nc.scalar.copy(
                         out=woven.rearrange("p (m s u) -> p m s u", m=RANKS, u=2), in_=turned[:].rearrange("p m u s -> p m s u")
                     )
-                    hidden.append(quantise_kept(woven.bitcast(BF16), "hidden%d" % e, "hidden%d" % e))
+                    hidden.append([plane[:] for plane in quantise_kept(woven.bitcast(BF16), "hidden%d" % e, "hidden%d" % e)])
             if is_up:
                 up_banks = banks
             else:
                 gate_banks = banks
 
-        raw2 = raws.tile([P, E, PACK * N], F32, name="raw", align_bytes=64)
-        order = (0, 1, 3, 2)
-        for place, e in enumerate(order):
-            nc.sync.dma_start(out=raw2[:, place, :], in_=w2[e].rearrange("(p j) n -> p (j n)", j=PACK))
-        rounded2 = keep.tile([P, E - 1, PACK * N], BF16, name="last_pass2", align_bytes=64)
-        for place in range(E - 1):
-            cast_down(nc.scalar.copy, rounded2[:, place, :], raw2[:, place, :])
+        wide = raws.tile([P, 10 * C], F32, name="raw", align_bytes=64)[:]
+        down_scales = keep.tile([P, E * N], U8, name="down_scales", align_bytes=64)[:]
+        rounded = {e: keep.tile([P, PACK * N], BF16, name="rounded%d" % e, align_bytes=64)[:] for e in (3, 2)}
+        last_codes = keep.tile([P, C], U32, name="last_codes", align_bytes=64)[:]
+        last_scales = keep.tile([P, C], U8, name="last_scales", align_bytes=64)[:]
+        raw2 = {
+            0: wide[:, : 2 * C],
+            1: wide[:, 2 * C : 4 * C],
+            3: wide[:, 6 * C + 3 * HALF // 2 : 8 * C + 3 * HALF // 2],
+            2: keep.tile([P, PACK * N], F32, name="raw_last", align_bytes=64)[:],
+        }
+        for e in (0, 1, 3, 2):
+            nc.sync.dma_start(out=raw2[e], in_=w2[e].rearrange("(p j) n -> p (j n)", j=PACK))
+        rounded_pair = keep.tile([P, 2 * PACK * N], BF16, name="last_pass2", align_bytes=64)[:]
+        for e in range(2):
+            cast_down(nc.scalar.copy, rounded_pair[:, e * PACK * N : (e + 1) * PACK * N], raw2[e])
+        cast_down(nc.scalar.copy, rounded[3], raw2[3])
 
         values = grouped[:, RANKS * H :].rearrange("p (m c) -> p m c", m=RANKS)
         turned = [psum_y.tile([P, 2, HALF], F32, name="turned") for m in range(RANKS)]
-        for half in range(2):
-            cols = slice(half * H // 2, (half + 1) * H // 2)
-            for m in range(RANKS):
-                sums = up_banks[half][:, m * H // 2 : (m + 1) * H // 2]
-                nc.vector.tensor_tensor(out=values[:, m, cols], in0=sums, in1=acts[m][:, cols], op=MULT)
+        gates = passes[0][:, : RANKS * H].rearrange("p (m c) -> p m c", m=RANKS)
+        for bank, (c0, c1) in zip(up_banks, LAST_PIECES):
+            for ranks in ([slice(0, RANKS)] if c1 < H else [slice(m, m + 1) for m in range(RANKS)]):
+                nc.vector.tensor_tensor(out=values[:, ranks, c0:c1], in0=bank[:, ranks, :], in1=gates[:, ranks, c0:c1], op=MULT)
         for m in range(RANKS):
             turn(turned[m][:], values[:, m, :])
-        down_codes = keep.tile([P, E * N], U32, name="last_pass0", align_bytes=64)
-        down_scales = keep.tile([P, E * N], U8, name="down_scales", align_bytes=64)
+        down_codes = keep.tile([P, E * N], U32, name="last_pass0", align_bytes=64)[:]
 
-        def quantise_down(place, rounded):
-            cols = slice(place * N, place * N + rounded.shape[1] // PACK)
-            nc.vector.quantize_mx(out=down_codes[:, cols].bitcast(FP8X4), scales=down_scales[:, cols], in_=rounded)
+        def quantise_down(e, values):
+            cols = slice(e * N, e * N + values.shape[1] // PACK)
+            nc.vector.quantize_mx(out=down_codes[:, cols].bitcast(FP8X4), scales=down_scales[:, cols], in_=values)
 
-        quantise_down(0, rounded2[:, :2, :].rearrange("p e x -> p (e x)"))
-        quantise_down(2, rounded2[:, 2, :])
-        cast_down(nc.vector.tensor_copy, values[:, 0, :], raw2[:, E - 1, :])
-        quantise_down(E - 1, values[:, 0, :])
-        down = {
-            e: [plane[:, place * N : (place + 1) * N] for plane in (down_codes, down_scales)] for place, e in enumerate(order)
-        }
-        woven = [keep.tile([P, HALF * 2], F32, name="woven%d" % m, align_bytes=64) for m in range(RANKS)]
+        quantise_down(0, rounded_pair)
+        quantise_down(3, rounded[3])
+        cast_down(nc.vector.tensor_copy, rounded[2], raw2[2])
+        quantise_down(2, rounded[2])
+        down = [[plane[:, e * N : (e + 1) * N] for plane in (down_codes, down_scales)] for e in range(E)]
+        woven = [wide[:, (6 + m) * C : (7 + m) * C] for m in range(RANKS)]
         for m in range(RANKS):
-            copy = nc.scalar.copy if m == 0 else nc.vector.tensor_copy
-            copy(out=woven[m][:].rearrange("p (s u) -> p s u", u=2), in_=turned[m][:].rearrange("p u s -> p s u"))
-        last = [quantise_kept(woven[m][:].bitcast(BF16), "last%d" % m, "last%d" % m) for m in range(RANKS)]
+            nc.scalar.copy(out=woven[m].rearrange("p (s u) -> p s u", u=2), in_=turned[m][:].rearrange("p u s -> p s u"))
+        last = [[plane[:, m * HALF : (m + 1) * HALF] for plane in (last_codes, last_scales)] for m in range(RANKS)]
+        for m in range(RANKS):
+            nc.vector.quantize_mx(out=last[m][0].bitcast(FP8X4), scales=last[m][1], in_=woven[m].bitcast(BF16))
 
         by_rank = out.rearrange("n (m x) -> n m x", m=RANKS)
-        early = keep.tile([P, RANKS, 2, HALF], F32, name="early")
+        early = wide[:, 8 * C :].rearrange("p (m e u) -> p m e u", m=RANKS, e=2)
         y = psum.tile([P, 2, C], F32, name="gate0")
         for e in range(2):
             second_layer(y[:, e, :], down[e], hidden[e])
-        nc.scalar.copy(out=early[:], in_=y[:].rearrange("p e (m u) -> p m e u", m=RANKS))
-        nc.sync.dma_start(out=by_rank[:, :, :C], in_=early[:].rearrange("p m e u -> p m (e u)"))
+        nc.scalar.copy(out=early, in_=y[:].rearrange("p e (m u) -> p m e u", m=RANKS))
+        nc.sync.dma_start(out=by_rank[:, :, :C], in_=early.rearrange("p m e u -> p m (e u)"))
         late = keep.tile([P, RANKS, 2, HALF], F32, name="late")
         y = psum.tile([P, C], F32, name="gate1")
-        second_layer(y[:], down[E - 2], hidden[E - 2])
+        second_layer(y[:], down[2], hidden[2])
         nc.scalar.copy(out=late[:, :, 0, :], in_=y[:].rearrange("p (m u) -> p m u", m=RANKS))
-        for m in range(RANKS):
-            copy = nc.scalar.copy if m == 0 else nc.vector.tensor_copy
-            y = psum_y.tile([P, HALF], F32, name="y")
-            second_layer(y[:], down[E - 1], last[m])
+        for m, copy in enumerate((nc.scalar.copy, nc.vector.tensor_copy)):
+            y = psum.tile([P, HALF], F32, name="up%d" % m)
+            second_layer(y[:], down[3], last[m])
             copy(out=late[:, m, 1, :], in_=y[:])
             nc.sync.dma_start(out=by_rank[:, m, C:], in_=late[:, m, :, :].rearrange("p e u -> p (e u)"))

@@ -28,7 +28,7 @@ GATE_SHARES = (0, 48, 64)
 UP_SHARE = 72
 LAST_SHARE = 88
 PIECE_SHARE = 40
-LAST_PIECES = ((0, H // 2), (H // 2, H - N), (H - N, H))
+LAST_PIECES = ((0, N), (N, H - N), (H - N, H))
 
 
 def tile_moe_pke_glu_gelu_kernel(tc, x_words, x_scales, w1, w3, w2, offs, out):
@@ -109,19 +109,18 @@ def tile_moe_pke_glu_gelu_kernel(tc, x_words, x_scales, w1, w3, w2, offs, out):
                 nc.vector.quantize_mx(out=codes.bitcast(FP8X4), scales=scales, in_=grouped)
                 return [codes[:, c0:c1] for c0, c1 in LAST_PIECES]
             src, final = raw_pass
-            nc.scalar.copy(out=dst[:, share:64, :, :], in_=src[:, share:64, :, :])
-            nc.vector.tensor_copy(out=dst[:, :share, :, :], in_=src[:, :share, :, :])
+            for g0 in (0, 32):
+                nc.vector.tensor_copy(out=dst[:, g0 : g0 + 32, :, :], in_=src[:, g0 : g0 + 32, :, :])
             nc.scalar.copy(out=dst[:, 64:96, :, :], in_=src[:, 64:96, :, :])
             piece_codes = []
             for c0, c1 in LAST_PIECES:
-                if c1 == H - N:
-                    nc.vector.tensor_copy(out=dst[:, 96:, :, :], in_=final)
-                    piece_codes.append(keep.tile([P, N], U32, name="last_piece", align_bytes=64)[:])
-                else:
-                    piece_codes.append(codes[:, c0:c1])
-                nc.vector.quantize_mx(
-                    out=piece_codes[-1].bitcast(FP8X4), scales=scales[:, c0:c1], in_=grouped[:, PACK * c0 : PACK * c1]
-                )
+                if c1 == H:
+                    nc.scalar.copy(out=dst[:, 96:, :, :], in_=final)
+                piece_codes.append(codes[:, c0:c1])
+                for c in range(c0, c1, N):
+                    nc.vector.quantize_mx(
+                        out=codes[:, c : c + N].bitcast(FP8X4), scales=scales[:, c : c + N], in_=grouped[:, PACK * c : PACK * (c + N)]
+                    )
             return piece_codes
 
         def product(sums, e, m, o, codes, scales, start, stop):
@@ -142,9 +141,11 @@ def tile_moe_pke_glu_gelu_kernel(tc, x_words, x_scales, w1, w3, w2, offs, out):
                     product(banks[m][:], e, m, o, codes, scales, o == 0, o == PASSES - 1)
                 return
             for bank, piece, (c0, c1) in zip(banks, piece_codes, LAST_PIECES):
-                for m in range(RANKS):
-                    start, stop = o == 0 and m == 0, o == PASSES - 1 and m == RANKS - 1
-                    product(bank[:, m, :], e, m, o, piece, scales[:, c0:c1], start, stop)
+                step = c1 - c0
+                for c in range(c0, c1, step):
+                    for m in range(RANKS):
+                        start, stop = o == 0 and m == 0, o == PASSES - 1 and m == RANKS - 1 and c + step == c1
+                        product(bank[:, m, c - c0 : c - c0 + step], e, m, o, codes[:, c : c + step], scales[:, c : c + step], start, stop)
 
         def turn(turned, values):
             pairs = values.bitcast(F32)
@@ -241,7 +242,7 @@ def tile_moe_pke_glu_gelu_kernel(tc, x_words, x_scales, w1, w3, w2, offs, out):
             cast_down(nc.scalar.copy, rounded_pair[:, e * PACK * N : (e + 1) * PACK * N], raw2[e])
         cast_down(nc.scalar.copy, rounded[3], raw2[3])
 
-        values = grouped[:, RANKS * H :].rearrange("p (m c) -> p m c", m=RANKS)
+        values = ring.tile([P, RANKS, H], BF16, name="values", bufs=1)
         turned = [psum_y.tile([P, 2, HALF], F32, name="turned") for m in range(RANKS)]
         gates = passes[0][:, : RANKS * H].rearrange("p (m c) -> p m c", m=RANKS)
         for bank, (c0, c1) in zip(up_banks, LAST_PIECES):
@@ -258,28 +259,29 @@ def tile_moe_pke_glu_gelu_kernel(tc, x_words, x_scales, w1, w3, w2, offs, out):
         quantise_down(0, rounded_pair)
         quantise_down(3, rounded[3])
         cast_down(nc.vector.tensor_copy, rounded[2], raw2[2])
-        quantise_down(2, rounded[2])
         down = [[plane[:, e * N : (e + 1) * N] for plane in (down_codes, down_scales)] for e in range(E)]
         woven = [wide[:, (6 + m) * C : (7 + m) * C] for m in range(RANKS)]
         for m in range(RANKS):
             nc.scalar.copy(out=woven[m].rearrange("p (s u) -> p s u", u=2), in_=turned[m][:].rearrange("p u s -> p s u"))
         last = [[plane[:, m * HALF : (m + 1) * HALF] for plane in (last_codes, last_scales)] for m in range(RANKS)]
         for m in range(RANKS):
+            if m:
+                quantise_down(2, rounded[2])
             nc.vector.quantize_mx(out=last[m][0].bitcast(FP8X4), scales=last[m][1], in_=woven[m].bitcast(BF16))
 
         by_rank = out.rearrange("n (m x) -> n m x", m=RANKS)
-        early = wide[:, 8 * C :].rearrange("p (m e u) -> p m e u", m=RANKS, e=2)
-        y = psum.tile([P, 2, C], F32, name="gate0")
         for e in range(2):
-            second_layer(y[:, e, :], down[e], hidden[e])
-        nc.scalar.copy(out=early, in_=y[:].rearrange("p e (m u) -> p m e u", m=RANKS))
-        nc.sync.dma_start(out=by_rank[:, :, :C], in_=early.rearrange("p m e u -> p m (e u)"))
+            y = psum.tile([P, C], F32, name="gate%d" % e)
+            second_layer(y[:], down[e], hidden[e])
+            early = wide[:, (8 + e) * C : (9 + e) * C]
+            nc.scalar.copy(out=early, in_=y[:])
+            nc.sync.dma_start(out=by_rank[:, :, e * HALF : (e + 1) * HALF], in_=early.rearrange("p (m u) -> p m u", m=RANKS))
         late = keep.tile([P, RANKS, 2, HALF], F32, name="late")
-        y = psum.tile([P, C], F32, name="gate1")
+        y = psum_y.tile([P, C], F32, name="y")
         second_layer(y[:], down[2], hidden[2])
         nc.scalar.copy(out=late[:, :, 0, :], in_=y[:].rearrange("p (m u) -> p m u", m=RANKS))
-        for m, copy in enumerate((nc.scalar.copy, nc.vector.tensor_copy)):
+        for m in range(RANKS):
             y = psum.tile([P, HALF], F32, name="up%d" % m)
             second_layer(y[:], down[3], last[m])
-            copy(out=late[:, m, 1, :], in_=y[:])
+            nc.vector.tensor_copy(out=late[:, m, 1, :], in_=y[:])
             nc.sync.dma_start(out=by_rank[:, m, C:], in_=late[:, m, :, :].rearrange("p e u -> p (e u)"))

from contextlib import ExitStack

import concourse.mybir as mybir
from concourse.masks import make_identity

K, T, E, C, H, N = 1536, 1024, 4, 256, 512, 128
RANKS = 2
FLOPS = 2 * E * C * (2 * K * H + H * N)

F32 = mybir.dt.float32
BF16 = mybir.dt.bfloat16
I32 = mybir.dt.int32
U32 = mybir.dt.uint32
U16 = mybir.dt.uint16
U8 = mybir.dt.uint8
FP8X4 = mybir.dt.float8_e4m3fn_x4
GELU = mybir.ActivationFunctionType.Gelu_apprx_tanh
MULT = mybir.AluOpType.mult

P = 128
PACK = 4
K_PASS = P * PACK
PASSES = K // K_PASS
HALF = C // RANKS
MATRICES = 2 * E
WHOLE = 2
GATE_SHARES = (0, 48, 64)
UP_SHARE = 72
LAST_SHARE = 88
PIECE_SHARE = 40
LAST_PIECES = ((0, N), (N, H - N), (H - N, H))


def tile_moe_pke_glu_gelu_kernel(tc, x_words, x_scales, w1, w3, w2, offs, out):
    nc = tc.nc
    with ExitStack() as ctx:
        keep = ctx.enter_context(tc.tile_pool(name="keep", bufs=1))
        raws = ctx.enter_context(tc.tile_pool(name="raws", bufs=4))
        ring = ctx.enter_context(tc.tile_pool(name="ring", bufs=4))
        psum = ctx.enter_context(tc.psum_pool(name="psum", bufs=1))
        psum_y = ctx.enter_context(tc.psum_pool(name="psum_y", bufs=2))

        def weight_rows(index):
            return (w1, w3)[index % 2][index // 2].rearrange("(o p j) c -> p o (j c)", o=PASSES, j=PACK)

        first_raw = raws.tile([P, PASSES, PACK * H], F32, name="raw", align_bytes=64)
        nc.sync.dma_start(out=first_raw[:, 0, :], in_=weight_rows(0)[:, 0, :])
        offsets = keep.tile([P, E * C // 16], U16, name="offsets")
        nc.sync.dma_start(offsets[:], offs)
        words_hbm = x_words.rearrange("o p t r -> p o (t r)").bitcast(I32)
        first_words = keep.tile([P, T], I32, name="first_words", align_bytes=64)
        nc.sync.dma_start(out=first_words[:], in_=words_hbm[:, 0, :])
        nc.sync.dma_start(out=first_raw[:, 1, :], in_=weight_rows(0)[:, 1, :])

        token_scales = keep.tile([P, T], U8, name="token_scales", align_bytes=64)
        nc.vector.memset(token_scales[:].bitcast(I32), 0)
        landed_scales = keep.tile([P, T // 4], I32, name="landed_scales")
        for q in range(4):
            live = slice(32 * q, 32 * q + 4 * PASSES)
            nc.sync.dma_start(out=landed_scales[live, :], in_=x_scales[:, 4 * q : 4 * q + 4, :].bitcast(I32))
            nc.vector.tensor_copy(out=token_scales[live, :].bitcast(I32), in_=landed_scales[live, :])

        later_words = keep.tile([P, PASSES - 1, T], I32, name="later_words", align_bytes=64)
        nc.sync.dma_start(out=later_words[:], in_=words_hbm[:, 1:, :])
        nc.sync.dma_start(out=first_raw[:, 2, :], in_=weight_rows(0)[:, 2, :])
        token_words = [first_words[:]] + [later_words[:, o, :] for o in range(PASSES - 1)]

        identity = keep.tile([P, P], F32, name="identity")
        make_identity(nc, identity[:])

        slot_words = [keep.tile([P, E * C], U32, name="slot_words%d" % o, align_bytes=64) for o in range(PASSES)]
        slot_scales = keep.tile([P, E * C], U8, name="slot_scales", align_bytes=64)

        def gather(gathered, window, e):
            picks = offsets[:, e * C // 16 : (e + 1) * C // 16]
            nc.vector.tensor_copy(gathered[:, e * C : (e + 1) * C], window.indirect(picks))

        def load(index):
            rows = weight_rows(index)
            if index == MATRICES - 1:
                passes = [keep.tile([P, PACK * H], F32, name="last_pass%d" % o, align_bytes=64)[:] for o in range(PASSES - 1)]
                for o in range(PASSES - 1):
                    nc.sync.dma_start(out=passes[o], in_=rows[:, o, :])
                last = rows[:, PASSES - 1, :].rearrange("p (j c) -> p j c", j=PACK)
                landed = []
                for name, c0, c1 in (("last_pass2", 0, H - N), ("last_piece", H - N, H)):
                    piece = keep.tile([P, PACK, c1 - c0], F32, name=name, align_bytes=64)
                    nc.sync.dma_start(out=piece[:], in_=last[:, :, c0:c1])
                    landed.append(piece[:].rearrange("p j (c i) -> p c j i", i=4))
                return passes + [landed]
            raw = raws.tile([P, PASSES, PACK * H], F32, name="raw", align_bytes=64)
            if index < WHOLE:
                cuts = [(0, PASSES)]
            elif index == WHOLE:
                cuts = [(0, PASSES - 1), (PASSES - 1, PASSES)]
            else:
                cuts = [(o, o + 1) for o in range(PASSES)]
            for o0, o1 in cuts:
                nc.sync.dma_start(out=raw[:, o0:o1, :], in_=rows[:, o0:o1, :])
            return [raw[:, o, :] for o in range(PASSES)]

        def quantise(raw_pass, grouped, codes, scales, share, in_halves):
            dst = grouped.rearrange("p (c i j) -> p c j i", i=4, j=PACK)
            if not in_halves:
                src = raw_pass.rearrange("p (j c i) -> p c j i", j=PACK, i=4)
                nc.scalar.copy(out=dst[:, share:, :, :], in_=src[:, share:, :, :])
                if share:
                    nc.vector.tensor_copy(out=dst[:, :share, :, :], in_=src[:, :share, :, :])
                nc.vector.quantize_mx(out=codes.bitcast(FP8X4), scales=scales, in_=grouped)
                return [codes[:, c0:c1] for c0, c1 in LAST_PIECES]
            src, final = raw_pass
            for g0 in (0, 32):
                nc.vector.tensor_copy(out=dst[:, g0 : g0 + 32, :, :], in_=src[:, g0 : g0 + 32, :, :])
            nc.scalar.copy(out=dst[:, 64:96, :, :], in_=src[:, 64:96, :, :])
            piece_codes = []
            for c0, c1 in LAST_PIECES:
                if c1 == H:
                    nc.scalar.copy(out=dst[:, 96:, :, :], in_=final)
                piece_codes.append(codes[:, c0:c1])
                for c in range(c0, c1, N):
                    nc.vector.quantize_mx(
                        out=codes[:, c : c + N].bitcast(FP8X4), scales=scales[:, c : c + N], in_=grouped[:, PACK * c : PACK * (c + N)]
                    )
            return piece_codes

        def product(sums, e, m, o, codes, scales, start, stop):
            cols = slice(e * C + m * HALF, e * C + (m + 1) * HALF)
            nc.tensor.matmul_mx(
                out=sums,
                lhsT=slot_words[o][:, cols].bitcast(FP8X4),
                lhsT_scale=slot_scales[4 * o : P, cols],
                rhs=codes.bitcast(FP8X4),
                rhs_scale=scales,
                start=start,
                stop=stop,
            )

        def multiply(banks, e, o, codes, scales, by_halves, piece_codes):
            if not by_halves:
                for m in range(RANKS):
                    product(banks[m][:], e, m, o, codes, scales, o == 0, o == PASSES - 1)
                return
            for bank, piece, (c0, c1) in zip(banks, piece_codes, LAST_PIECES):
                step = c1 - c0
                for c in range(c0, c1, step):
                    for m in range(RANKS):
                        start, stop = o == 0 and m == 0, o == PASSES - 1 and m == RANKS - 1 and c + step == c1
                        product(bank[:, m, c - c0 : c - c0 + step], e, m, o, codes[:, c : c + step], scales[:, c : c + step], start, stop)

        def turn(turned, values):
            pairs = values.bitcast(F32)
            for u in range(2):
                nc.tensor.transpose(turned[:, u, :], pairs[:, u : H // 2 : 2], identity[:])

        def quantise_kept(values, name, codes_tag):
            width = values.shape[1] // PACK
            codes = keep.tile([P, width], U32, name=codes_tag, align_bytes=64)
            scales = keep.tile([P, width], U8, name=name + "_scales", align_bytes=64)
            nc.vector.quantize_mx(out=codes[:].bitcast(FP8X4), scales=scales[:], in_=values)
            return codes, scales

        def cast_down(copy, grouped2, raw_rows):
            copy(
                out=grouped2.rearrange("p (c i j) -> p c j i", i=4, j=PACK),
                in_=raw_rows.rearrange("p (j c i) -> p c j i", i=4, j=PACK),
            )

        def second_layer(y, weights, slots):
            nc.tensor.matmul_mx(
                out=y,
                lhsT=weights[0].bitcast(FP8X4),
                lhsT_scale=weights[1],
                rhs=slots[0].bitcast(FP8X4),
                rhs_scale=slots[1],
                start=True,
                stop=True,
            )

        hidden = []
        acts = {}
        for index in range(MATRICES):
            e, is_up = divmod(index, 2)
            is_last = index == MATRICES - 1
            passes = load(index) if index else [first_raw[:, o, :] for o in range(PASSES)]
            if is_last:
                banks = [psum.tile([P, RANKS, c1 - c0], F32, name="up%d" % m) for m, (c0, c1) in enumerate(LAST_PIECES[:2])]
                banks.append(psum_y.tile([P, RANKS, N], F32, name="y"))
            else:
                banks = [psum.tile([P, H], F32, name="%s%d" % (("gate", "up")[is_up], m)) for m in range(RANKS)]
            for o in range(PASSES):
                grouped = ring.tile([P, PACK * H], BF16, name="grouped", align_bytes=64)
                codes = ring.tile([P, H], U32, name="codes", align_bytes=64)
                scales = ring.tile([P, H], U8, name="scales", align_bytes=64)
                if is_last and o > 0:
                    share = LAST_SHARE if o == 1 else PIECE_SHARE
                else:
                    share = UP_SHARE if is_up else GATE_SHARES[o]
                if o == 0 and not is_up and e > 0:
                    turned = psum_y.tile([P, RANKS, 2, HALF], F32, name="turned")
                    values = ring.tile([P, RANKS, H], BF16, name="values", bufs=1)
                    for m in range(RANKS):
                        nc.vector.tensor_tensor(out=values[:, m, :], in0=up_banks[m][:], in1=acts[m], op=MULT)
                piece_codes = quantise(passes[o], grouped[:], codes[:], scales[:], share, is_last and o == PASSES - 1)
                if index == 0 or (is_up and not is_last):
                    gather(slot_words[o], token_words[o].bitcast(U32), e + is_up)
                    if o == 0:
                        gather(slot_scales, token_scales[:], e + is_up)
                multiply(banks, e, o, codes[:], scales[:], is_last, piece_codes)
                for m in range(RANKS):
                    if is_up and o == (0 if is_last else m):
                        acts[m] = passes[o][:, m * H : (m + 1) * H]
                        nc.scalar.activation(out=acts[m], in_=gate_banks[m][:], func=GELU)
                if o == 0 and not is_up and e > 0:
                    for m in range(RANKS):
                        turn(turned[:, m, :, :], values[:, m, :])
                if o == 1 and not is_up and e > 0:
                    woven = passes[o][:, :H]
                    nc.scalar.copy(
                        out=woven.rearrange("p (m s u) -> p m s u", m=RANKS, u=2), in_=turned[:].rearrange("p m u s -> p m s u")
                    )
                    hidden.append([plane[:] for plane in quantise_kept(woven.bitcast(BF16), "hidden%d" % e, "hidden%d" % e)])
            if is_up:
                up_banks = banks
            else:
                gate_banks = banks

        wide = raws.tile([P, 10 * C], F32, name="raw", align_bytes=64)[:]
        down_scales = keep.tile([P, E * N], U8, name="down_scales", align_bytes=64)[:]
        rounded = {e: keep.tile([P, PACK * N], BF16, name="rounded%d" % e, align_bytes=64)[:] for e in (3, 2)}
        last_codes = keep.tile([P, C], U32, name="last_codes", align_bytes=64)[:]
        last_scales = keep.tile([P, C], U8, name="last_scales", align_bytes=64)[:]
        raw2 = {
            0: wide[:, : 2 * C],
            1: wide[:, 2 * C : 4 * C],
            3: wide[:, 6 * C + 3 * HALF // 2 : 8 * C + 3 * HALF // 2],
            2: keep.tile([P, PACK * N], F32, name="raw_last", align_bytes=64)[:],
        }
        for e in (0, 1, 3, 2):
            nc.sync.dma_start(out=raw2[e], in_=w2[e].rearrange("(p j) n -> p (j n)", j=PACK))
        rounded_pair = keep.tile([P, 2 * PACK * N], BF16, name="last_pass2", align_bytes=64)[:]
        for e in range(2):
            cast_down(nc.scalar.copy, rounded_pair[:, e * PACK * N : (e + 1) * PACK * N], raw2[e])
        cast_down(nc.scalar.copy, rounded[3], raw2[3])

        values = ring.tile([P, RANKS, H], BF16, name="values", bufs=1)
        turned = [psum_y.tile([P, 2, HALF], F32, name="turned") for m in range(RANKS)]
        gates = passes[0][:, : RANKS * H].rearrange("p (m c) -> p m c", m=RANKS)
        for bank, (c0, c1) in zip(up_banks, LAST_PIECES):
            for ranks in ([slice(0, RANKS)] if c1 < H else [slice(m, m + 1) for m in range(RANKS)]):
                nc.vector.tensor_tensor(out=values[:, ranks, c0:c1], in0=bank[:, ranks, :], in1=gates[:, ranks, c0:c1], op=MULT)
        for m in range(RANKS):
            turn(turned[m][:], values[:, m, :])
        down_codes = keep.tile([P, E * N], U32, name="last_pass0", align_bytes=64)[:]

        def quantise_down(e, values):
            cols = slice(e * N, e * N + values.shape[1] // PACK)
            nc.vector.quantize_mx(out=down_codes[:, cols].bitcast(FP8X4), scales=down_scales[:, cols], in_=values)

        quantise_down(0, rounded_pair)
        quantise_down(3, rounded[3])
        cast_down(nc.vector.tensor_copy, rounded[2], raw2[2])
        down = [[plane[:, e * N : (e + 1) * N] for plane in (down_codes, down_scales)] for e in range(E)]
        woven = [wide[:, (6 + m) * C : (7 + m) * C] for m in range(RANKS)]
        for m in range(RANKS):
            nc.scalar.copy(out=woven[m].rearrange("p (s u) -> p s u", u=2), in_=turned[m][:].rearrange("p u s -> p s u"))
        last = [[plane[:, m * HALF : (m + 1) * HALF] for plane in (last_codes, last_scales)] for m in range(RANKS)]
        for m in range(RANKS):
            if m:
                quantise_down(2, rounded[2])
            nc.vector.quantize_mx(out=last[m][0].bitcast(FP8X4), scales=last[m][1], in_=woven[m].bitcast(BF16))

        by_rank = out.rearrange("n (m x) -> n m x", m=RANKS)
        for e in range(2):
            y = psum.tile([P, C], F32, name="gate%d" % e)
            second_layer(y[:], down[e], hidden[e])
            early = wide[:, (8 + e) * C : (9 + e) * C]
            nc.scalar.copy(out=early, in_=y[:])
            nc.sync.dma_start(out=by_rank[:, :, e * HALF : (e + 1) * HALF], in_=early.rearrange("p (m u) -> p m u", m=RANKS))
        late = keep.tile([P, RANKS, 2, HALF], F32, name="late")
        y = psum_y.tile([P, C], F32, name="y")
        second_layer(y[:], down[2], hidden[2])
        nc.scalar.copy(out=late[:, :, 0, :], in_=y[:].rearrange("p (m u) -> p m u", m=RANKS))
        for m in range(RANKS):
            y = psum.tile([P, HALF], F32, name="up%d" % m)
            second_layer(y[:], down[3], last[m])
            nc.vector.tensor_copy(out=late[:, m, 1, :], in_=y[:])
            nc.sync.dma_start(out=by_rank[:, m, C:], in_=late[:, m, :, :].rearrange("p e u -> p (e u)"))
